import numpy as np
import ml_dtypes


def mxq(x, axis, fmt="e4m3"):
    dtype, down = {"e4m3": (ml_dtypes.float8_e4m3fn, 7), "e5m2": (ml_dtypes.float8_e5m2, 14)}[fmt]
    v = np.moveaxis(np.asarray(x, np.float32).astype(ml_dtypes.bfloat16).astype(np.float64), axis, -1)
    blocks = v.reshape(v.shape[:-1] + (-1, 32))
    amax = np.abs(blocks).max(-1, keepdims=True)
    byte = np.maximum(np.where(amax > 0, np.frexp(amax)[1] - 1 + 127, 0) - down, 1)
    scale = np.exp2(byte - 127.0)
    codes = (blocks / scale).astype(np.float32).astype(dtype).astype(np.float64)
    return np.moveaxis((codes * scale).reshape(v.shape), -1, axis)


WIDE = False


def mx_kscale(k):
    if not WIDE:
        return np.ones(k)
    levels = np.array([10, -10, 5, -5, 0])
    if k % 512:
        return np.exp2(np.random.permutation(np.resize(levels, k // 32))).repeat(32)
    a = np.empty((k // 512, 16))
    for p in range(k // 512):
        a[p, :8] = np.random.permutation(np.resize(levels, 8))
        for g in range(8):
            far = levels[np.abs(levels - a[p, g]) >= 10]
            a[p, g + 8] = far[np.random.randint(len(far))]
    return np.exp2(a.ravel()).repeat(32)


def f64(x):
    return np.asarray(x).astype(np.float64)


def striped(idx):
    return np.tile(np.asarray(idx).reshape(-1, 16).T, (8, 1)).astype(np.uint16)


def unstriped(offs):
    return offs[:16].T.reshape(-1).astype(np.int64)


E2M1 = np.array([0.0, 0.5, 1.0, 1.5, 2.0, 3.0, 4.0, 6.0, -0.0, -0.5, -1.0, -1.5, -2.0, -3.0, -4.0, -6.0])


def pack_weight(w, fmt):
    k, n = w.shape
    w = f64(np.asarray(w, np.float32).astype(ml_dtypes.bfloat16)).reshape(k // 32, 32, n)
    amax = np.abs(w).max(1)
    if fmt == "e4m3":
        byte = np.frexp(amax)[1] - 1 + 127 - 7
    else:
        mant, ex = np.frexp(amax / 6.0)
        byte = np.where(mant > 0.5, ex, ex - 1) + 127
    byte = np.clip(np.where(amax > 0, byte, 1), 1, 254)
    scaled = (w * np.exp2(127.0 - byte)[:, None, :]).reshape(k, n).astype(np.float32)
    by_word = np.ascontiguousarray(scaled.reshape(k // 512, 128, 4, n).transpose(0, 1, 3, 2))
    if fmt == "e4m3":
        words = by_word.astype(ml_dtypes.float8_e4m3fn).view(np.uint8)
    else:
        c = by_word.astype(ml_dtypes.float4_e2m1fn).view(np.uint8) & 0xF
        words = (c[..., 0::2] | (c[..., 1::2] << 4)).reshape(k // 512, 128, 2 * n)
    return np.ascontiguousarray(words), np.ascontiguousarray(byte.astype(np.uint8).reshape(k // 512, 16, n))


def unpack_weight(words, scales, fmt):
    g, _, n = scales.shape
    words = np.ascontiguousarray(words).reshape(g, 128, n, -1)
    if fmt == "e4m3":
        vals = words.view(ml_dtypes.float8_e4m3fn).astype(np.float64)
    else:
        nib = np.empty((g, 128, n, 4), np.uint8)
        nib[..., 0::2] = words & 0xF
        nib[..., 1::2] = words >> 4
        vals = E2M1[nib]
    vals = vals * np.repeat(np.exp2(scales.astype(np.float64) - 127.0), 8, axis=1)[..., None]
    return vals.transpose(0, 1, 3, 2).reshape(g * 512, n)


B, N, T, D, NQ = 1, 512, 4096, 1024, 256


def setup_inputs():
    n = np.random.standard_normal
    idx = np.random.permutation(T)[:B * N]
    s = mx_kscale(D)[:, None]
    kp = pack_weight(n((D, T)) / s, "e2m1")
    return {
        "qT": (n((B, D, NQ)) * s * (1.00 / np.sqrt(D))).astype(np.float32),
        "k_words": np.ascontiguousarray(kp[0].reshape(1, 2, 128, T, 2).transpose(0, 2, 3, 1, 4)).reshape(1, 128, T, 4),
        "k_scales": kp[1],
        "kb": np.tile(n(4096), (128, 1)).astype(np.float32),
        "ls": (np.random.uniform(8.5, 9.0, (B, NQ, 1))).astype(np.float32),
        "offs": striped(idx),
    }


def reference(qT, k_words, k_scales, kb, ls, offs):
    idx = unstriped(offs)
    pick = lambda x, which: x[:, which].reshape(x.shape[0], B, -1).transpose(1, 0, 2)
    k = unpack_weight(k_words.reshape(1, 128, T, 2, 2).transpose(0, 3, 1, 2, 4).reshape(2, 128, 2 * T), k_scales, "e2m1")
    kg = pick(k, idx)
    qq = mxq(f64(qT), 1, "e4m3")
    a = qq.transpose(0, 2, 1) @ kg
    y = a + pick(f64(kb), idx)[:, :1, :] - f64(ls)
    return y

@@ -1,0 +1,128 @@
+from contextlib import ExitStack
+
+import concourse.mybir as mybir
+from concourse.masks import make_identity
+
+F32 = mybir.dt.float32
+BF16 = mybir.dt.bfloat16
+I32 = mybir.dt.int32
+U32 = mybir.dt.uint32
+U16 = mybir.dt.uint16
+U8 = mybir.dt.uint8
+FP8X4 = mybir.dt.float8_e4m3fn_x4
+FP4X4 = mybir.dt.float4_e2m1fn_x4
+ALU = mybir.AluOpType
+
+P = 128
+SLOTS, VOCAB, D, NQ = 512, 4096, 1024, 256
+PASSES = D // 512
+BLOCKS = NQ // P
+KB_ROW = 4
+
+FLOPS = 2 * NQ * SLOTS * D
+
+
+def tile_attend_logprob_topk_kernel(tc, qT, k_words, k_scales, kb, ls, offs, out):
+    nc = tc.nc
+    with ExitStack() as ctx:
+        keep = ctx.enter_context(tc.tile_pool(name="keep", bufs=1))
+        psum = ctx.enter_context(tc.psum_pool(name="psum", bufs=1))
+
+        offsets = keep.tile([P, SLOTS // 16], U16, name="offsets")
+        nc.sync.dma_start(offsets[:], offs)
+
+        q_raw = [keep.tile([P, 4, NQ], F32, name=f"q_raw{o}") for o in range(PASSES)]
+        words = keep.tile([P, VOCAB], U32, name="words", align_bytes=64)
+        q_rows = qT[0].rearrange("(o p j) q -> o p j q", o=PASSES, j=4)
+        nc.sync.dma_start(out=q_raw[0][:], in_=q_rows[0])
+        nc.sync.dma_start(out=words[:].bitcast(I32),
+                          in_=k_words[0].rearrange("p t b -> p (t b)").bitcast(I32))
+        nc.sync.dma_start(out=q_raw[1][:], in_=q_rows[1])
+
+        lse = keep.tile([P, BLOCKS], F32, name="lse")
+        with nc.allow_non_contiguous_dma(reason="one float32 for each query row"):
+            nc.scalar.dma_start(out=lse[:], in_=ls[0].rearrange("(b p) o -> p (b o)", p=P))
+
+        scale_rows = keep.tile([P, PASSES, VOCAB], U8, name="scale_rows", align_bytes=64)
+        scale_flat = scale_rows[:].rearrange("p o t -> p (o t)")
+        nc.vector.memset(scale_flat.bitcast(I32), 0)
+        nc.scalar.dma_start(out=scale_rows[0:P:8, :, :].bitcast(I32),
+                            in_=k_scales.rearrange("o f t -> f o t").bitcast(I32))
+
+        kb_row = keep.tile([P, VOCAB], F32, name="kb_row", align_bytes=64)
+        nc.vector.memset(kb_row[:], 0.0)
+        nc.scalar.dma_start(out=kb_row[KB_ROW:KB_ROW + 1, :], in_=kb[0:1, :])
+
+        ident = keep.tile([P, P], F32, name="ident")
+        make_identity(nc, ident[:])
+
+        grouped = [keep.tile([P, NQ, 4], BF16, name=f"grouped{o}", align_bytes=64) for o in range(PASSES)]
+        q_codes = [keep.tile([P, NQ], U32, name=f"q_codes{o}", align_bytes=64) for o in range(PASSES)]
+        q_scales = [keep.tile([P, NQ], U8, name=f"q_scales{o}", align_bytes=64) for o in range(PASSES)]
+
+        def cast(o, cols):
+            nc.scalar.copy(out=grouped[o][:, cols, :].rearrange("p (c i) t -> p c t i", i=4),
+                           in_=q_raw[o][:, :, cols].rearrange("p t (c i) -> p c t i", i=4))
+
+        def quantize(o, cols):
+            nc.vector.quantize_mx(out=q_codes[o][:, cols].bitcast(FP8X4), scales=q_scales[o][:, cols],
+                                  in_=grouped[o][:, cols, :].rearrange("p w t -> p (w t)"))
+
+        cast(0, slice(0, NQ))
+
+        picked_scales = keep.tile([P, PASSES * SLOTS], U8, name="picked_scales", align_bytes=64)
+        for o in range(PASSES):
+            nc.vector.tensor_copy(picked_scales[:, o * SLOTS:(o + 1) * SLOTS],
+                                  scale_rows[:, o, :].indirect(offsets[:]))
+        key_scales = keep.tile([P, PASSES * SLOTS], U8, name="key_scales", align_bytes=64)
+        nc.vector.tensor_copy(key_scales[:].bitcast(I32), picked_scales[:].bitcast(I32))
+        for j in range(1, 4):
+            nc.scalar.dma_start(out=key_scales[j:P:32, :].bitcast(I32),
+                                in_=picked_scales[8 * j:P:32, :].bitcast(I32))
+
+        picked_kb = keep.tile([P, SLOTS], F32, name="picked_kb")
+        nc.vector.tensor_copy(picked_kb[:], kb_row[:].indirect(offsets[:]))
+        quantize(0, slice(0, NQ))
+
+        turned = psum.tile([P, SLOTS // P, P], F32, name="turned")
+        for m in range(SLOTS // P):
+            nc.tensor.transpose(turned[:, m, :], picked_kb[:, m * P:(m + 1) * P], ident[:])
+        kb_cols = keep.tile([P, SLOTS // P], F32, name="kb_cols")
+        nc.scalar.copy(out=kb_cols[:], in_=turned[:, :, KB_ROW])
+        spread = psum.tile([P, SLOTS], F32, name="spread")
+        for m in range(SLOTS // P):
+            nc.tensor.transpose(spread[:, m * P:(m + 1) * P],
+                                kb_cols[:, m:m + 1].to_broadcast([P, P]), ident[:])
+        kb_all = keep.tile([P, SLOTS], F32, name="kb_all")
+        nc.scalar.copy(out=kb_all[:], in_=spread[:])
+
+        picked_words = keep.tile([P, SLOTS], U32, name="picked_words", align_bytes=64)
+        nc.vector.tensor_copy(picked_words[:], words[:].indirect(offsets[:]))
+        halves = picked_words[:].bitcast(U16).rearrange("p (n h) -> p h n", h=2)
+        key_codes = [keep.tile([P, SLOTS], U16, name=f"key_codes{o}", align_bytes=64) for o in range(PASSES)]
+        for o in range(PASSES):
+            nc.vector.tensor_copy(key_codes[o][:], halves[:, o, :])
+
+        acc = [psum.tile([P, SLOTS], F32, name=f"acc{b}") for b in range(BLOCKS)]
+
+        def multiply(o, b):
+            cols = slice(b * P, (b + 1) * P)
+            nc.tensor.matmul_mx(out=acc[b][:], lhsT=q_codes[o][:, cols].bitcast(FP8X4),
+                                lhsT_scale=q_scales[o][:, cols],
+                                rhs=key_codes[o][:].bitcast(FP4X4),
+                                rhs_scale=key_scales[:, o * SLOTS:(o + 1) * SLOTS],
+                                start=(o == 0), stop=(o == PASSES - 1))
+
+        for b in range(BLOCKS):
+            multiply(0, b)
+        for b in range(BLOCKS):
+            cast(1, slice(b * P, (b + 1) * P))
+        for b in range(BLOCKS):
+            quantize(1, slice(b * P, (b + 1) * P))
+        for b in range(BLOCKS):
+            multiply(1, b)
+        for b in range(BLOCKS):
+            result = keep.tile([P, SLOTS], F32, name=f"result{b}")
+            nc.vector.scalar_tensor_tensor(out=result[:], in0=acc[b][:], scalar=lse[:, b:b + 1],
+                                           in1=kb_all[:], op0=ALU.subtract, op1=ALU.add)
+            nc.sync.dma_start(out=out[0, b * P:(b + 1) * P, :], in_=result[:])

@@ -17,7 +17,8 @@ P = 128
 SLOTS, VOCAB, D, NQ = 512, 4096, 1024, 256
 PASSES = D // 512
 BLOCKS = NQ // P
-KB_ROW = 4
+KB_ROW = P - 1
+SCALE_ROWS = 16 * PASSES
 
 FLOPS = 2 * NQ * SLOTS * D
 
@@ -31,6 +32,12 @@ def tile_attend_logprob_topk_kernel(tc, qT, k_words, k_scales, kb, ls, offs, out
         offsets = keep.tile([P, SLOTS // 16], U16, name="offsets")
         nc.sync.dma_start(offsets[:], offs)
 
+        scale_rows = keep.tile([P, VOCAB], U8, name="scale_rows", align_bytes=64)
+        nc.sync.dma_start(out=scale_rows[0:SCALE_ROWS, :].bitcast(I32),
+                          in_=k_scales.rearrange("o f t -> (o f) t").bitcast(I32))
+        kb_row = keep.tile([P, VOCAB], F32, name="kb_row", align_bytes=64)
+        nc.sync.dma_start(out=kb_row[KB_ROW:KB_ROW + 1, :], in_=kb[0:1, :])
+
         q_raw = [keep.tile([P, 4, NQ], F32, name=f"q_raw{o}") for o in range(PASSES)]
         words = keep.tile([P, VOCAB], U32, name="words", align_bytes=64)
         q_rows = qT[0].rearrange("(o p j) q -> o p j q", o=PASSES, j=4)
@@ -42,16 +49,14 @@ def tile_attend_logprob_topk_kernel(tc, qT, k_words, k_scales, kb, ls, offs, out
         lse = keep.tile([P, BLOCKS], F32, name="lse")
         with nc.allow_non_contiguous_dma(reason="one float32 for each query row"):
             nc.scalar.dma_start(out=lse[:], in_=ls[0].rearrange("(b p) o -> p (b o)", p=P))
+        neg_lse = keep.tile([P, BLOCKS], F32, name="neg_lse")
+        nc.scalar.mul(neg_lse[:], lse[:], -1.0)
 
-        scale_rows = keep.tile([P, PASSES, VOCAB], U8, name="scale_rows", align_bytes=64)
-        scale_flat = scale_rows[:].rearrange("p o t -> p (o t)")
-        nc.vector.memset(scale_flat.bitcast(I32), 0)
-        nc.scalar.dma_start(out=scale_rows[0:P:8, :, :].bitcast(I32),
-                            in_=k_scales.rearrange("o f t -> f o t").bitcast(I32))
-
-        kb_row = keep.tile([P, VOCAB], F32, name="kb_row", align_bytes=64)
-        nc.vector.memset(kb_row[:], 0.0)
-        nc.scalar.dma_start(out=kb_row[KB_ROW:KB_ROW + 1, :], in_=kb[0:1, :])
+        nc.vector.memset(scale_rows[32:64, :].bitcast(I32), 0)
+        nc.vector.memset(scale_rows[64:P, :].bitcast(I32), 0)
+        nc.vector.memset(kb_row[0:KB_ROW, :].bitcast(I32), 0)
+        key_scales = [keep.tile([P, SLOTS], U8, name=f"key_scales{o}", align_bytes=64) for o in range(PASSES)]
+        nc.vector.memset(key_scales[1][:].bitcast(I32), 0)
 
         ident = keep.tile([P, P], F32, name="ident")
         make_identity(nc, ident[:])
@@ -70,25 +75,24 @@ def tile_attend_logprob_topk_kernel(tc, qT, k_words, k_scales, kb, ls, offs, out
 
         cast(0, slice(0, NQ))
 
-        picked_scales = keep.tile([P, PASSES * SLOTS], U8, name="picked_scales", align_bytes=64)
-        for o in range(PASSES):
-            nc.vector.tensor_copy(picked_scales[:, o * SLOTS:(o + 1) * SLOTS],
-                                  scale_rows[:, o, :].indirect(offsets[:]))
-        key_scales = keep.tile([P, PASSES * SLOTS], U8, name="key_scales", align_bytes=64)
-        nc.vector.tensor_copy(key_scales[:].bitcast(I32), picked_scales[:].bitcast(I32))
-        for j in range(1, 4):
-            nc.scalar.dma_start(out=key_scales[j:P:32, :].bitcast(I32),
-                                in_=picked_scales[8 * j:P:32, :].bitcast(I32))
+        picked_scales = keep.tile([P, SLOTS], U8, name="picked_scales", align_bytes=64)
+        nc.vector.tensor_copy(picked_scales[:], scale_rows[:].indirect(offsets[:]))
+        nc.vector.tensor_copy(key_scales[0][:].bitcast(I32), picked_scales[:].bitcast(I32))
+        for group in range(1, SCALE_ROWS // 4):
+            o, quadrant = divmod(group, 4)
+            queue = nc.gpsimd if group == SCALE_ROWS // 4 - 1 else nc.scalar
+            queue.dma_start(out=key_scales[o][32 * quadrant:32 * quadrant + 4, :].bitcast(I32),
+                            in_=picked_scales[4 * group:4 * group + 4, :].bitcast(I32))
 
         picked_kb = keep.tile([P, SLOTS], F32, name="picked_kb")
         nc.vector.tensor_copy(picked_kb[:], kb_row[:].indirect(offsets[:]))
-        quantize(0, slice(0, NQ))
 
         turned = psum.tile([P, SLOTS // P, P], F32, name="turned")
         for m in range(SLOTS // P):
             nc.tensor.transpose(turned[:, m, :], picked_kb[:, m * P:(m + 1) * P], ident[:])
         kb_cols = keep.tile([P, SLOTS // P], F32, name="kb_cols")
-        nc.scalar.copy(out=kb_cols[:], in_=turned[:, :, KB_ROW])
+        nc.vector.tensor_copy(out=kb_cols[:], in_=turned[:, :, KB_ROW])
+        quantize(0, slice(0, NQ))
         spread = psum.tile([P, SLOTS], F32, name="spread")
         for m in range(SLOTS // P):
             nc.tensor.transpose(spread[:, m * P:(m + 1) * P],
@@ -110,19 +114,18 @@ def tile_attend_logprob_topk_kernel(tc, qT, k_words, k_scales, kb, ls, offs, out
             nc.tensor.matmul_mx(out=acc[b][:], lhsT=q_codes[o][:, cols].bitcast(FP8X4),
                                 lhsT_scale=q_scales[o][:, cols],
                                 rhs=key_codes[o][:].bitcast(FP4X4),
-                                rhs_scale=key_scales[:, o * SLOTS:(o + 1) * SLOTS],
+                                rhs_scale=key_scales[o][:],
                                 start=(o == 0), stop=(o == PASSES - 1))
 
-        for b in range(BLOCKS):
-            multiply(0, b)
         for b in range(BLOCKS):
             cast(1, slice(b * P, (b + 1) * P))
         for b in range(BLOCKS):
             quantize(1, slice(b * P, (b + 1) * P))
         for b in range(BLOCKS):
-            multiply(1, b)
+            for o in range(PASSES):
+                multiply(o, b)
         for b in range(BLOCKS):
             result = keep.tile([P, SLOTS], F32, name=f"result{b}")
-            nc.vector.scalar_tensor_tensor(out=result[:], in0=acc[b][:], scalar=lse[:, b:b + 1],
-                                           in1=kb_all[:], op0=ALU.subtract, op1=ALU.add)
+            nc.vector.scalar_tensor_tensor(out=result[:], in0=acc[b][:], scalar=neg_lse[:, b:b + 1],
+                                           in1=kb_all[:], op0=ALU.add, op1=ALU.add)
             nc.sync.dma_start(out=out[0, b * P:(b + 1) * P, :], in_=result[:])

@@ -18,6 +18,9 @@ SLOTS, VOCAB, D, NQ = 512, 4096, 1024, 256
 PASSES = D // 512
 BLOCKS = NQ // P
 KB_ROW = P - 1
+KB_SPLIT = 1600
+WARM_UPS = 16
+PIECE = 256
 SCALE_ROWS = 16 * PASSES
 
 FLOPS = 2 * NQ * SLOTS * D
@@ -35,16 +38,16 @@ def tile_attend_logprob_topk_kernel(tc, qT, k_words, k_scales, kb, ls, offs, out
         scale_rows = keep.tile([P, VOCAB], U8, name="scale_rows", align_bytes=64)
         nc.sync.dma_start(out=scale_rows[0:SCALE_ROWS, :].bitcast(I32),
                           in_=k_scales.rearrange("o f t -> (o f) t").bitcast(I32))
-        kb_row = keep.tile([P, VOCAB], F32, name="kb_row", align_bytes=64)
-        nc.sync.dma_start(out=kb_row[KB_ROW:KB_ROW + 1, :], in_=kb[0:1, :])
+        kb_row = keep.tile([P, VOCAB + 8], F32, name="kb_row", tag="kb_row", align_bytes=64)
+        nc.sync.dma_start(out=kb_row[KB_ROW:KB_ROW + 1, 0:VOCAB], in_=kb[0:1, :])
 
         q_raw = [keep.tile([P, 4, NQ], F32, name=f"q_raw{o}") for o in range(PASSES)]
         words = keep.tile([P, VOCAB], U32, name="words", align_bytes=64)
         q_rows = qT[0].rearrange("(o p j) q -> o p j q", o=PASSES, j=4)
-        nc.sync.dma_start(out=q_raw[0][:], in_=q_rows[0])
         nc.sync.dma_start(out=words[:].bitcast(I32),
                           in_=k_words[0].rearrange("p t b -> p (t b)").bitcast(I32))
-        nc.sync.dma_start(out=q_raw[1][:], in_=q_rows[1])
+        for o in range(PASSES):
+            nc.sync.dma_start(out=q_raw[o][:], in_=q_rows[o])
 
         lse = keep.tile([P, BLOCKS], F32, name="lse")
         with nc.allow_non_contiguous_dma(reason="one float32 for each query row"):
@@ -52,55 +55,57 @@ def tile_attend_logprob_topk_kernel(tc, qT, k_words, k_scales, kb, ls, offs, out
         neg_lse = keep.tile([P, BLOCKS], F32, name="neg_lse")
         nc.scalar.mul(neg_lse[:], lse[:], -1.0)
 
-        nc.vector.memset(scale_rows[32:64, :].bitcast(I32), 0)
-        nc.vector.memset(scale_rows[64:P, :].bitcast(I32), 0)
-        nc.vector.memset(kb_row[0:KB_ROW, :].bitcast(I32), 0)
+        nc.gpsimd.memset(kb_row[0:KB_ROW, 0:KB_SPLIT], 0.0)
+        nc.vector.memset(kb_row[0:KB_ROW, KB_SPLIT:VOCAB + 1], 0.0)
         key_scales = [keep.tile([P, SLOTS], U8, name=f"key_scales{o}", align_bytes=64) for o in range(PASSES)]
-        nc.vector.memset(key_scales[1][:].bitcast(I32), 0)
 
         ident = keep.tile([P, P], F32, name="ident")
         make_identity(nc, ident[:])
+        nc.gpsimd.memset(scale_rows[32:64, :].bitcast(I32), 0)
+        nc.gpsimd.memset(scale_rows[64:P, :].bitcast(I32), 0)
 
-        grouped = [keep.tile([P, NQ, 4], BF16, name=f"grouped{o}", align_bytes=64) for o in range(PASSES)]
+        grouped = []
         q_codes = [keep.tile([P, NQ], U32, name=f"q_codes{o}", align_bytes=64) for o in range(PASSES)]
         q_scales = [keep.tile([P, NQ], U8, name=f"q_scales{o}", align_bytes=64) for o in range(PASSES)]
 
-        def cast(o, cols):
-            nc.scalar.copy(out=grouped[o][:, cols, :].rearrange("p (c i) t -> p c t i", i=4),
+        def cast(o, cols, copy):
+            copy(out=grouped[o][:, cols, :].rearrange("p (c i) t -> p c t i", i=4),
                            in_=q_raw[o][:, :, cols].rearrange("p t (c i) -> p c t i", i=4))
 
         def quantize(o, cols):
             nc.vector.quantize_mx(out=q_codes[o][:, cols].bitcast(FP8X4), scales=q_scales[o][:, cols],
                                   in_=grouped[o][:, cols, :].rearrange("p w t -> p (w t)"))
 
-        cast(0, slice(0, NQ))
-
-        picked_scales = keep.tile([P, SLOTS], U8, name="picked_scales", align_bytes=64)
-        nc.vector.tensor_copy(picked_scales[:], scale_rows[:].indirect(offsets[:]))
-        nc.vector.tensor_copy(key_scales[0][:].bitcast(I32), picked_scales[:].bitcast(I32))
-        for group in range(1, SCALE_ROWS // 4):
-            o, quadrant = divmod(group, 4)
-            queue = nc.gpsimd if group == SCALE_ROWS // 4 - 1 else nc.scalar
-            queue.dma_start(out=key_scales[o][32 * quadrant:32 * quadrant + 4, :].bitcast(I32),
-                            in_=picked_scales[4 * group:4 * group + 4, :].bitcast(I32))
-
-        picked_kb = keep.tile([P, SLOTS], F32, name="picked_kb")
-        nc.vector.tensor_copy(picked_kb[:], kb_row[:].indirect(offsets[:]))
-
+        picked_kb = keep.tile([P, SLOTS], F32, name="picked_kb", tag="picked", align_bytes=64)
+        nc.vector.tensor_copy(picked_kb[:], kb_row[:, 0:VOCAB].indirect(offsets[:]))
         turned = psum.tile([P, SLOTS // P, P], F32, name="turned")
         for m in range(SLOTS // P):
             nc.tensor.transpose(turned[:, m, :], picked_kb[:, m * P:(m + 1) * P], ident[:])
         kb_cols = keep.tile([P, SLOTS // P], F32, name="kb_cols")
         nc.vector.tensor_copy(out=kb_cols[:], in_=turned[:, :, KB_ROW])
-        quantize(0, slice(0, NQ))
         spread = psum.tile([P, SLOTS], F32, name="spread")
         for m in range(SLOTS // P):
             nc.tensor.transpose(spread[:, m * P:(m + 1) * P],
                                 kb_cols[:, m:m + 1].to_broadcast([P, P]), ident[:])
         kb_all = keep.tile([P, SLOTS], F32, name="kb_all")
         nc.scalar.copy(out=kb_all[:], in_=spread[:])
+        warm = psum.tile([P, SLOTS], F32, name="warm")
+        for i in range(WARM_UPS):
+            m = i % (SLOTS // P)
+            nc.tensor.transpose(warm[:, m * P:(m + 1) * P],
+                                kb_cols[:, m:m + 1].to_broadcast([P, P]), ident[:])
 
-        picked_words = keep.tile([P, SLOTS], U32, name="picked_words", align_bytes=64)
+        nc.gpsimd.memset(key_scales[1][:].bitcast(I32), 0)
+        picked_scales = keep.tile([P, SLOTS], U8, name="picked_scales", tag="kb_row", align_bytes=64)
+        nc.vector.tensor_copy(picked_scales[:], scale_rows[:].indirect(offsets[:]))
+        nc.vector.tensor_copy(key_scales[0][:].bitcast(I32), picked_scales[:].bitcast(I32))
+        for group in range(1, SCALE_ROWS // 4):
+            o, quadrant = divmod(group, 4)
+            nc.sync.dma_start(out=key_scales[o][32 * quadrant:32 * quadrant + 4, :].bitcast(I32),
+                            in_=picked_scales[4 * group:4 * group + 4, :].bitcast(I32))
+
+
+        picked_words = keep.tile([P, SLOTS], U32, name="picked_words", tag="picked", align_bytes=64)
         nc.vector.tensor_copy(picked_words[:], words[:].indirect(offsets[:]))
         halves = picked_words[:].bitcast(U16).rearrange("p (n h) -> p h n", h=2)
         key_codes = [keep.tile([P, SLOTS], U16, name=f"key_codes{o}", align_bytes=64) for o in range(PASSES)]
@@ -117,15 +122,24 @@ def tile_attend_logprob_topk_kernel(tc, qT, k_words, k_scales, kb, ls, offs, out
                                 rhs_scale=key_scales[o][:],
                                 start=(o == 0), stop=(o == PASSES - 1))
 
-        for b in range(BLOCKS):
-            cast(1, slice(b * P, (b + 1) * P))
-        for b in range(BLOCKS):
-            quantize(1, slice(b * P, (b + 1) * P))
+        for o in range(PASSES):
+            grouped.append(keep.tile([P, NQ, 4], BF16, name=f"grouped{o}", tag=f"grouped{o}", align_bytes=64))
+        first, second = slice(0, P), slice(P, NQ)
+        cast(0, first, nc.scalar.copy)
+        cast(0, second, nc.scalar.copy)
+        quantize(0, first)
+        cast(1, first, nc.vector.tensor_copy)
+        cast(1, second, nc.scalar.copy)
+        quantize(1, first)
+        quantize(0, second)
+        quantize(1, second)
         for b in range(BLOCKS):
             for o in range(PASSES):
                 multiply(o, b)
         for b in range(BLOCKS):
-            result = keep.tile([P, SLOTS], F32, name=f"result{b}")
-            nc.vector.scalar_tensor_tensor(out=result[:], in0=acc[b][:], scalar=neg_lse[:, b:b + 1],
-                                           in1=kb_all[:], op0=ALU.add, op1=ALU.add)
-            nc.sync.dma_start(out=out[0, b * P:(b + 1) * P, :], in_=result[:])
+            for c in range(0, SLOTS, PIECE):
+                cols = slice(c, c + PIECE)
+                result = keep.tile([P, PIECE], F32, name=f"result{b}_{c}")
+                nc.vector.scalar_tensor_tensor(out=result[:], in0=acc[b][:, cols], scalar=neg_lse[:, b:b + 1],
+                                               in1=kb_all[:, cols], op0=ALU.add, op1=ALU.add)
+                nc.sync.dma_start(out=out[0, b * P:(b + 1) * P, cols], in_=result[:])

@@ -18,10 +18,10 @@ SLOTS, VOCAB, D, NQ = 512, 4096, 1024, 256
 PASSES = D // 512
 BLOCKS = NQ // P
 KB_ROW = P - 1
-KB_SPLIT = 1600
-WARM_UPS = 16
 PIECE = 256
 SCALE_ROWS = 16 * PASSES
+KB_SPLIT = 1600
+EARLY, LATE = 1, 0
 
 FLOPS = 2 * NQ * SLOTS * D
 
@@ -35,84 +35,90 @@ def tile_attend_logprob_topk_kernel(tc, qT, k_words, k_scales, kb, ls, offs, out
         offsets = keep.tile([P, SLOTS // 16], U16, name="offsets")
         nc.sync.dma_start(offsets[:], offs)
 
-        scale_rows = keep.tile([P, VOCAB], U8, name="scale_rows", align_bytes=64)
-        nc.sync.dma_start(out=scale_rows[0:SCALE_ROWS, :].bitcast(I32),
+        scale_rows = keep.tile([P, VOCAB + 32], U8, name="scale_rows", align_bytes=64)
+        nc.sync.dma_start(out=scale_rows[0:SCALE_ROWS, 0:VOCAB].bitcast(I32),
                           in_=k_scales.rearrange("o f t -> (o f) t").bitcast(I32))
         kb_row = keep.tile([P, VOCAB + 8], F32, name="kb_row", tag="kb_row", align_bytes=64)
-        nc.sync.dma_start(out=kb_row[KB_ROW:KB_ROW + 1, 0:VOCAB], in_=kb[0:1, :])
+        nc.sync.dma_start(out=kb_row[KB_ROW:P, 0:VOCAB], in_=kb[0:1, :])
 
-        q_raw = [keep.tile([P, 4, NQ], F32, name=f"q_raw{o}") for o in range(PASSES)]
         words = keep.tile([P, VOCAB], U32, name="words", align_bytes=64)
-        q_rows = qT[0].rearrange("(o p j) q -> o p j q", o=PASSES, j=4)
         nc.sync.dma_start(out=words[:].bitcast(I32),
                           in_=k_words[0].rearrange("p t b -> p (t b)").bitcast(I32))
-        for o in range(PASSES):
+        q_raw = [keep.tile([P, 4, NQ], F32, name=f"q_raw{o}", tag=f"q_raw{o}") for o in range(PASSES)]
+        q_rows = qT[0].rearrange("(o p j) q -> o p j q", o=PASSES, j=4)
+        for o in (EARLY, LATE):
             nc.sync.dma_start(out=q_raw[o][:], in_=q_rows[o])
 
-        lse = keep.tile([P, BLOCKS], F32, name="lse")
-        with nc.allow_non_contiguous_dma(reason="one float32 for each query row"):
-            nc.scalar.dma_start(out=lse[:], in_=ls[0].rearrange("(b p) o -> p (b o)", p=P))
-        neg_lse = keep.tile([P, BLOCKS], F32, name="neg_lse")
-        nc.scalar.mul(neg_lse[:], lse[:], -1.0)
-
-        nc.gpsimd.memset(kb_row[0:KB_ROW, 0:KB_SPLIT], 0.0)
-        nc.vector.memset(kb_row[0:KB_ROW, KB_SPLIT:VOCAB + 1], 0.0)
-        key_scales = [keep.tile([P, SLOTS], U8, name=f"key_scales{o}", align_bytes=64) for o in range(PASSES)]
+        ls_rows = keep.tile([P, P], F32, name="ls_rows")
+        nc.scalar.dma_start(out=ls_rows[P - BLOCKS:P, :], in_=ls[0].rearrange("(b p) o -> b (p o)", p=P))
 
         ident = keep.tile([P, P], F32, name="ident")
         make_identity(nc, ident[:])
-        nc.gpsimd.memset(scale_rows[32:64, :].bitcast(I32), 0)
-        nc.gpsimd.memset(scale_rows[64:P, :].bitcast(I32), 0)
+        nc.vector.memset(ls_rows[0:P - BLOCKS, :], 0.0)
+        nc.vector.memset(scale_rows[64:P, 0:VOCAB + 4].bitcast(I32), 0)
+        nc.gpsimd.memset(scale_rows[32:64, 0:VOCAB].bitcast(I32), 0)
+        key_scales = {EARLY: keep.tile([P, SLOTS], U8, name="early_scales", align_bytes=64)}
+        nc.gpsimd.memset(key_scales[EARLY][:].bitcast(I32), 0)
+        nc.gpsimd.memset(kb_row[0:KB_ROW, 0:KB_SPLIT], 0.0)
+        nc.vector.memset(kb_row[0:KB_ROW, KB_SPLIT:VOCAB + 1], 0.0)
 
-        grouped = []
-        q_codes = [keep.tile([P, NQ], U32, name=f"q_codes{o}", align_bytes=64) for o in range(PASSES)]
-        q_scales = [keep.tile([P, NQ], U8, name=f"q_scales{o}", align_bytes=64) for o in range(PASSES)]
+        ls_turned = psum.tile([P, P], F32, name="ls_turned")
+        neg_rows = keep.tile([P, P], F32, name="neg_rows")
+        nc.scalar.mul(neg_rows[:], ls_rows[:], -1.0)
+        nc.tensor.transpose(ls_turned[:], neg_rows[:], ident[:])
+        neg_lse = keep.tile([P, BLOCKS], F32, name="neg_lse")
+        nc.scalar.copy(neg_lse[:], ls_turned[:, P - BLOCKS:P])
 
-        def cast(o, cols, copy):
-            copy(out=grouped[o][:, cols, :].rearrange("p (c i) t -> p c t i", i=4),
-                           in_=q_raw[o][:, :, cols].rearrange("p t (c i) -> p c t i", i=4))
+        picked_scales = keep.tile([P, SLOTS], U8, name="picked_scales", align_bytes=64)
+        nc.vector.tensor_copy(picked_scales[:], scale_rows[:, 0:VOCAB].indirect(offsets[:]))
 
-        def quantize(o, cols):
-            nc.vector.quantize_mx(out=q_codes[o][:, cols].bitcast(FP8X4), scales=q_scales[o][:, cols],
-                                  in_=grouped[o][:, cols, :].rearrange("p w t -> p (w t)"))
+        def place_scales(o, queue):
+            for quadrant in range(4):
+                group = 4 * o + quadrant
+                if group > 0:
+                    queue.dma_start(out=key_scales[o][32 * quadrant:32 * quadrant + 4, :].bitcast(I32),
+                                    in_=picked_scales[4 * group:4 * group + 4, :].bitcast(I32))
 
-        picked_kb = keep.tile([P, SLOTS], F32, name="picked_kb", tag="picked", align_bytes=64)
+        place_scales(EARLY, nc.scalar)
+
+        picked_kb = keep.tile([P, SLOTS], F32, name="picked_kb")
         nc.vector.tensor_copy(picked_kb[:], kb_row[:, 0:VOCAB].indirect(offsets[:]))
+        key_scales[LATE] = keep.tile([P, SLOTS], U8, name="late_scales", tag="kb_row", align_bytes=64)
+        nc.vector.tensor_copy(key_scales[LATE][:].bitcast(I32), picked_scales[:].bitcast(I32))
+        place_scales(LATE, nc.sync)
+
         turned = psum.tile([P, SLOTS // P, P], F32, name="turned")
         for m in range(SLOTS // P):
             nc.tensor.transpose(turned[:, m, :], picked_kb[:, m * P:(m + 1) * P], ident[:])
         kb_cols = keep.tile([P, SLOTS // P], F32, name="kb_cols")
-        nc.vector.tensor_copy(out=kb_cols[:], in_=turned[:, :, KB_ROW])
+        nc.scalar.copy(out=kb_cols[:], in_=turned[:, :, KB_ROW])
         spread = psum.tile([P, SLOTS], F32, name="spread")
         for m in range(SLOTS // P):
             nc.tensor.transpose(spread[:, m * P:(m + 1) * P],
                                 kb_cols[:, m:m + 1].to_broadcast([P, P]), ident[:])
-        kb_all = keep.tile([P, SLOTS], F32, name="kb_all")
-        nc.scalar.copy(out=kb_all[:], in_=spread[:])
-        warm = psum.tile([P, SLOTS], F32, name="warm")
-        for i in range(WARM_UPS):
-            m = i % (SLOTS // P)
-            nc.tensor.transpose(warm[:, m * P:(m + 1) * P],
-                                kb_cols[:, m:m + 1].to_broadcast([P, P]), ident[:])
 
-        nc.gpsimd.memset(key_scales[1][:].bitcast(I32), 0)
-        picked_scales = keep.tile([P, SLOTS], U8, name="picked_scales", tag="kb_row", align_bytes=64)
-        nc.vector.tensor_copy(picked_scales[:], scale_rows[:].indirect(offsets[:]))
-        nc.vector.tensor_copy(key_scales[0][:].bitcast(I32), picked_scales[:].bitcast(I32))
-        for group in range(1, SCALE_ROWS // 4):
-            o, quadrant = divmod(group, 4)
-            nc.sync.dma_start(out=key_scales[o][32 * quadrant:32 * quadrant + 4, :].bitcast(I32),
-                            in_=picked_scales[4 * group:4 * group + 4, :].bitcast(I32))
-
-
-        picked_words = keep.tile([P, SLOTS], U32, name="picked_words", tag="picked", align_bytes=64)
+        picked_words = keep.tile([P, SLOTS], U32, name="picked_words", align_bytes=64)
         nc.vector.tensor_copy(picked_words[:], words[:].indirect(offsets[:]))
         halves = picked_words[:].bitcast(U16).rearrange("p (n h) -> p h n", h=2)
         key_codes = [keep.tile([P, SLOTS], U16, name=f"key_codes{o}", align_bytes=64) for o in range(PASSES)]
-        for o in range(PASSES):
+
+        grouped = [keep.tile([P, NQ, 4], BF16, name=f"grouped{o}", align_bytes=64) for o in range(PASSES)]
+        q_codes = [keep.tile([P, NQ], U32, name=f"q_codes{o}", align_bytes=64) for o in range(PASSES)]
+        q_scales = [keep.tile([P, NQ], U8, name=f"q_scales{o}", align_bytes=64) for o in range(PASSES)]
+        acc = [psum.tile([P, SLOTS], F32, name=f"acc{b}") for b in range(BLOCKS)]
+
+        def part(o):
             nc.vector.tensor_copy(key_codes[o][:], halves[:, o, :])
 
-        acc = [psum.tile([P, SLOTS], F32, name=f"acc{b}") for b in range(BLOCKS)]
+        def cast(o, b, copy):
+            cols = slice(b * P, (b + 1) * P)
+            copy(out=grouped[o][:, cols, :].rearrange("p (c i) t -> p c t i", i=4),
+                 in_=q_raw[o][:, :, cols].rearrange("p t (c i) -> p c t i", i=4))
+
+        def quantize(o, b):
+            cols = slice(b * P, (b + 1) * P)
+            nc.vector.quantize_mx(out=q_codes[o][:, cols].bitcast(FP8X4), scales=q_scales[o][:, cols],
+                                  in_=grouped[o][:, cols, :].rearrange("p w t -> p (w t)"))
 
         def multiply(o, b):
             cols = slice(b * P, (b + 1) * P)
@@ -120,21 +126,22 @@ def tile_attend_logprob_topk_kernel(tc, qT, k_words, k_scales, kb, ls, offs, out
                                 lhsT_scale=q_scales[o][:, cols],
                                 rhs=key_codes[o][:].bitcast(FP4X4),
                                 rhs_scale=key_scales[o][:],
-                                start=(o == 0), stop=(o == PASSES - 1))
+                                start=(o == EARLY), stop=(o == LATE))
 
-        for o in range(PASSES):
-            grouped.append(keep.tile([P, NQ, 4], BF16, name=f"grouped{o}", tag=f"grouped{o}", align_bytes=64))
-        first, second = slice(0, P), slice(P, NQ)
-        cast(0, first, nc.scalar.copy)
-        cast(0, second, nc.scalar.copy)
-        quantize(0, first)
-        cast(1, first, nc.vector.tensor_copy)
-        cast(1, second, nc.scalar.copy)
-        quantize(1, first)
-        quantize(0, second)
-        quantize(1, second)
-        for b in range(BLOCKS):
-            for o in range(PASSES):
+        part(EARLY)
+        cast(EARLY, 0, nc.scalar.copy)
+        cast(EARLY, 1, nc.scalar.copy)
+        quantize(EARLY, 0)
+        part(LATE)
+        quantize(EARLY, 1)
+        cast(LATE, 0, nc.vector.tensor_copy)
+        cast(LATE, 1, nc.scalar.copy)
+        kb_all = keep.tile([P, SLOTS], F32, name="kb_all", tag=f"q_raw{LATE}")
+        nc.scalar.copy(out=kb_all[:], in_=spread[:])
+        quantize(LATE, 0)
+        quantize(LATE, 1)
+        for o in (EARLY, LATE):
+            for b in range(BLOCKS):
                 multiply(o, b)
         for b in range(BLOCKS):
             for c in range(0, SLOTS, PIECE):

@@ -20,7 +20,7 @@ BLOCKS = NQ // P
 KB_ROW = P - 1
 PIECE = 256
 SCALE_ROWS = 16 * PASSES
-KB_SPLIT = 1600
+KB_SPLIT = 2112
 EARLY, LATE = 1, 0
 
 FLOPS = 2 * NQ * SLOTS * D
@@ -35,11 +35,11 @@ def tile_attend_logprob_topk_kernel(tc, qT, k_words, k_scales, kb, ls, offs, out
         offsets = keep.tile([P, SLOTS // 16], U16, name="offsets")
         nc.sync.dma_start(offsets[:], offs)
 
-        scale_rows = keep.tile([P, VOCAB + 32], U8, name="scale_rows", align_bytes=64)
-        nc.sync.dma_start(out=scale_rows[0:SCALE_ROWS, 0:VOCAB].bitcast(I32),
-                          in_=k_scales.rearrange("o f t -> (o f) t").bitcast(I32))
-        kb_row = keep.tile([P, VOCAB + 8], F32, name="kb_row", tag="kb_row", align_bytes=64)
+        kb_row = keep.tile([P, VOCAB + 16], F32, name="kb_row", align_bytes=64)
         nc.sync.dma_start(out=kb_row[KB_ROW:P, 0:VOCAB], in_=kb[0:1, :])
+        scale_rows = keep.tile([P, VOCAB + 64], U8, name="scale_rows", align_bytes=64)
+        nc.sync.dma_start(out=scale_rows[P - SCALE_ROWS:P, 0:VOCAB].bitcast(I32),
+                          in_=k_scales.rearrange("o f t -> f o t").bitcast(I32))
 
         words = keep.tile([P, VOCAB], U32, name="words", align_bytes=64)
         nc.sync.dma_start(out=words[:].bitcast(I32),
@@ -54,38 +54,18 @@ def tile_attend_logprob_topk_kernel(tc, qT, k_words, k_scales, kb, ls, offs, out
 
         ident = keep.tile([P, P], F32, name="ident")
         make_identity(nc, ident[:])
-        nc.vector.memset(ls_rows[0:P - BLOCKS, :], 0.0)
-        nc.vector.memset(scale_rows[64:P, 0:VOCAB + 4].bitcast(I32), 0)
-        nc.gpsimd.memset(scale_rows[32:64, 0:VOCAB].bitcast(I32), 0)
-        key_scales = {EARLY: keep.tile([P, SLOTS], U8, name="early_scales", align_bytes=64)}
-        nc.gpsimd.memset(key_scales[EARLY][:].bitcast(I32), 0)
+        nc.scalar.copy(ls_rows[0:P - BLOCKS, :], ident[0:P - BLOCKS, :])
+        nc.vector.memset(scale_rows[0:P - SCALE_ROWS, 0:VOCAB + 4].bitcast(I32), 0)
+        key_scales = keep.tile([P, PASSES * SLOTS], U8, name="key_scales", align_bytes=64)
+        nc.gpsimd.memset(key_scales[:].bitcast(I32), 0)
         nc.gpsimd.memset(kb_row[0:KB_ROW, 0:KB_SPLIT], 0.0)
         nc.vector.memset(kb_row[0:KB_ROW, KB_SPLIT:VOCAB + 1], 0.0)
 
         ls_turned = psum.tile([P, P], F32, name="ls_turned")
-        neg_rows = keep.tile([P, P], F32, name="neg_rows")
-        nc.scalar.mul(neg_rows[:], ls_rows[:], -1.0)
-        nc.tensor.transpose(ls_turned[:], neg_rows[:], ident[:])
-        neg_lse = keep.tile([P, BLOCKS], F32, name="neg_lse")
-        nc.scalar.copy(neg_lse[:], ls_turned[:, P - BLOCKS:P])
-
-        picked_scales = keep.tile([P, SLOTS], U8, name="picked_scales", align_bytes=64)
-        nc.vector.tensor_copy(picked_scales[:], scale_rows[:, 0:VOCAB].indirect(offsets[:]))
-
-        def place_scales(o, queue):
-            for quadrant in range(4):
-                group = 4 * o + quadrant
-                if group > 0:
-                    queue.dma_start(out=key_scales[o][32 * quadrant:32 * quadrant + 4, :].bitcast(I32),
-                                    in_=picked_scales[4 * group:4 * group + 4, :].bitcast(I32))
-
-        place_scales(EARLY, nc.scalar)
+        nc.tensor.transpose(ls_turned[:], ls_rows[:], ident[:])
 
         picked_kb = keep.tile([P, SLOTS], F32, name="picked_kb")
         nc.vector.tensor_copy(picked_kb[:], kb_row[:, 0:VOCAB].indirect(offsets[:]))
-        key_scales[LATE] = keep.tile([P, SLOTS], U8, name="late_scales", tag="kb_row", align_bytes=64)
-        nc.vector.tensor_copy(key_scales[LATE][:].bitcast(I32), picked_scales[:].bitcast(I32))
-        place_scales(LATE, nc.sync)
 
         turned = psum.tile([P, SLOTS // P, P], F32, name="turned")
         for m in range(SLOTS // P):
@@ -97,36 +77,35 @@ def tile_attend_logprob_topk_kernel(tc, qT, k_words, k_scales, kb, ls, offs, out
             nc.tensor.transpose(spread[:, m * P:(m + 1) * P],
                                 kb_cols[:, m:m + 1].to_broadcast([P, P]), ident[:])
 
+        picked_scales = keep.tile([P, SLOTS], U8, name="picked_scales", align_bytes=64)
+        nc.vector.tensor_copy(picked_scales[:], scale_rows[:, 0:VOCAB].indirect(offsets[:]))
+
+        for quadrant in range(4):
+            nc.scalar.dma_start(out=key_scales[32 * quadrant:32 * quadrant + 4, :].bitcast(I32),
+                                in_=picked_scales[96 + 8 * quadrant:96 + 8 * quadrant + 8, :].bitcast(I32))
+
+
         picked_words = keep.tile([P, SLOTS], U32, name="picked_words", align_bytes=64)
         nc.vector.tensor_copy(picked_words[:], words[:].indirect(offsets[:]))
         halves = picked_words[:].bitcast(U16).rearrange("p (n h) -> p h n", h=2)
         key_codes = [keep.tile([P, SLOTS], U16, name=f"key_codes{o}", align_bytes=64) for o in range(PASSES)]
 
-        grouped = [keep.tile([P, NQ, 4], BF16, name=f"grouped{o}", align_bytes=64) for o in range(PASSES)]
-        q_codes = [keep.tile([P, NQ], U32, name=f"q_codes{o}", align_bytes=64) for o in range(PASSES)]
-        q_scales = [keep.tile([P, NQ], U8, name=f"q_scales{o}", align_bytes=64) for o in range(PASSES)]
+        units = [(o, b) for o in (EARLY, LATE) for b in range(BLOCKS)]
+        grouped = {u: keep.tile([P, P, 4], BF16, name=f"grouped{u[0]}{u[1]}", align_bytes=64) for u in units}
+        q_codes = {u: keep.tile([P, P], U32, name=f"q_codes{u[0]}{u[1]}", align_bytes=64) for u in units}
+        q_scales = {u: keep.tile([P, P], U8, name=f"q_scales{u[0]}{u[1]}", align_bytes=64) for u in units}
         acc = [psum.tile([P, SLOTS], F32, name=f"acc{b}") for b in range(BLOCKS)]
 
         def part(o):
             nc.vector.tensor_copy(key_codes[o][:], halves[:, o, :])
 
         def cast(o, b, copy):
-            cols = slice(b * P, (b + 1) * P)
-            copy(out=grouped[o][:, cols, :].rearrange("p (c i) t -> p c t i", i=4),
-                 in_=q_raw[o][:, :, cols].rearrange("p t (c i) -> p c t i", i=4))
+            copy(out=grouped[o, b][:].rearrange("p (c i) t -> p c t i", i=4),
+                 in_=q_raw[o][:, :, b * P:(b + 1) * P].rearrange("p t (c i) -> p c t i", i=4))
 
         def quantize(o, b):
-            cols = slice(b * P, (b + 1) * P)
-            nc.vector.quantize_mx(out=q_codes[o][:, cols].bitcast(FP8X4), scales=q_scales[o][:, cols],
-                                  in_=grouped[o][:, cols, :].rearrange("p w t -> p (w t)"))
-
-        def multiply(o, b):
-            cols = slice(b * P, (b + 1) * P)
-            nc.tensor.matmul_mx(out=acc[b][:], lhsT=q_codes[o][:, cols].bitcast(FP8X4),
-                                lhsT_scale=q_scales[o][:, cols],
-                                rhs=key_codes[o][:].bitcast(FP4X4),
-                                rhs_scale=key_scales[o][:],
-                                start=(o == EARLY), stop=(o == LATE))
+            nc.vector.quantize_mx(out=q_codes[o, b][:].bitcast(FP8X4), scales=q_scales[o, b][:],
+                                  in_=grouped[o, b][:].rearrange("p w t -> p (w t)"))
 
         part(EARLY)
         cast(EARLY, 0, nc.scalar.copy)
@@ -136,17 +115,19 @@ def tile_attend_logprob_topk_kernel(tc, qT, k_words, k_scales, kb, ls, offs, out
         quantize(EARLY, 1)
         cast(LATE, 0, nc.vector.tensor_copy)
         cast(LATE, 1, nc.scalar.copy)
-        kb_all = keep.tile([P, SLOTS], F32, name="kb_all", tag=f"q_raw{LATE}")
-        nc.scalar.copy(out=kb_all[:], in_=spread[:])
         quantize(LATE, 0)
         quantize(LATE, 1)
-        for o in (EARLY, LATE):
-            for b in range(BLOCKS):
-                multiply(o, b)
+        kb_all = keep.tile([P, SLOTS], F32, name="kb_all", tag=f"q_raw{LATE}")
+        nc.scalar.copy(out=kb_all[:], in_=spread[:])
+        for o, b in units:
+            nc.tensor.matmul_mx(out=acc[b][:], lhsT=q_codes[o, b][:].bitcast(FP8X4), lhsT_scale=q_scales[o, b][:],
+                                rhs=key_codes[o][:].bitcast(FP4X4),
+                                rhs_scale=key_scales[:, o * SLOTS:(o + 1) * SLOTS],
+                                start=(o == EARLY), stop=(o == LATE))
         for b in range(BLOCKS):
             for c in range(0, SLOTS, PIECE):
                 cols = slice(c, c + PIECE)
                 result = keep.tile([P, PIECE], F32, name=f"result{b}_{c}")
-                nc.vector.scalar_tensor_tensor(out=result[:], in0=acc[b][:, cols], scalar=neg_lse[:, b:b + 1],
-                                               in1=kb_all[:, cols], op0=ALU.add, op1=ALU.add)
+                nc.vector.scalar_tensor_tensor(out=result[:], in0=acc[b][:, cols], scalar=ls_turned[:, P - BLOCKS + b:P - BLOCKS + b + 1],
+                                               in1=kb_all[:, cols], op0=ALU.subtract, op1=ALU.add)
                 nc.sync.dma_start(out=out[0, b * P:(b + 1) * P, cols], in_=result[:])

@@ -20,7 +20,9 @@ BLOCKS = NQ // P
 KB_ROW = P - 1
 PIECE = 256
 SCALE_ROWS = 16 * PASSES
-KB_SPLIT = 2112
+SCALE_BASE = 0
+KB_GPSIMD = 2816
+KB_PIECE = 512
 EARLY, LATE = 1, 0
 
 FLOPS = 2 * NQ * SLOTS * D
@@ -35,19 +37,14 @@ def tile_attend_logprob_topk_kernel(tc, qT, k_words, k_scales, kb, ls, offs, out
         offsets = keep.tile([P, SLOTS // 16], U16, name="offsets")
         nc.sync.dma_start(offsets[:], offs)
 
+        scale_rows = keep.tile([P, VOCAB + 64], U8, name="scale_rows", tag="shared", align_bytes=64)
+        nc.sync.dma_start(out=scale_rows[0:SCALE_ROWS, 0:VOCAB].bitcast(I32),
+                          in_=k_scales.rearrange("o f t -> f o t").bitcast(I32))
         kb_row = keep.tile([P, VOCAB + 16], F32, name="kb_row", align_bytes=64)
         nc.sync.dma_start(out=kb_row[KB_ROW:P, 0:VOCAB], in_=kb[0:1, :])
-        scale_rows = keep.tile([P, VOCAB + 64], U8, name="scale_rows", align_bytes=64)
-        nc.sync.dma_start(out=scale_rows[P - SCALE_ROWS:P, 0:VOCAB].bitcast(I32),
-                          in_=k_scales.rearrange("o f t -> f o t").bitcast(I32))
-
         words = keep.tile([P, VOCAB], U32, name="words", align_bytes=64)
         nc.sync.dma_start(out=words[:].bitcast(I32),
                           in_=k_words[0].rearrange("p t b -> p (t b)").bitcast(I32))
-        q_raw = [keep.tile([P, 4, NQ], F32, name=f"q_raw{o}", tag=f"q_raw{o}") for o in range(PASSES)]
-        q_rows = qT[0].rearrange("(o p j) q -> o p j q", o=PASSES, j=4)
-        for o in (EARLY, LATE):
-            nc.sync.dma_start(out=q_raw[o][:], in_=q_rows[o])
 
         ls_rows = keep.tile([P, P], F32, name="ls_rows")
         nc.scalar.dma_start(out=ls_rows[P - BLOCKS:P, :], in_=ls[0].rearrange("(b p) o -> b (p o)", p=P))
@@ -55,14 +52,27 @@ def tile_attend_logprob_topk_kernel(tc, qT, k_words, k_scales, kb, ls, offs, out
         ident = keep.tile([P, P], F32, name="ident")
         make_identity(nc, ident[:])
         nc.scalar.copy(ls_rows[0:P - BLOCKS, :], ident[0:P - BLOCKS, :])
-        nc.vector.memset(scale_rows[0:P - SCALE_ROWS, 0:VOCAB + 4].bitcast(I32), 0)
+        nc.vector.memset(scale_rows[64:P, 0:VOCAB + 4].bitcast(I32), 0)
+        nc.gpsimd.memset(scale_rows[32:64, 0:VOCAB].bitcast(I32), 0)
         key_scales = keep.tile([P, PASSES * SLOTS], U8, name="key_scales", align_bytes=64)
-        nc.gpsimd.memset(key_scales[:].bitcast(I32), 0)
-        nc.gpsimd.memset(kb_row[0:KB_ROW, 0:KB_SPLIT], 0.0)
-        nc.vector.memset(kb_row[0:KB_ROW, KB_SPLIT:VOCAB + 1], 0.0)
+        nc.vector.memset(key_scales[:].bitcast(I32), 0)
+        nc.vector.memset(kb_row[0:KB_ROW, KB_GPSIMD:VOCAB + 1], 0.0)
+        for c in range(0, KB_GPSIMD, KB_PIECE):
+            nc.gpsimd.memset(kb_row[0:KB_ROW, c:min(c + KB_PIECE, KB_GPSIMD)], 0.0)
 
         ls_turned = psum.tile([P, P], F32, name="ls_turned")
         nc.tensor.transpose(ls_turned[:], ls_rows[:], ident[:])
+
+        picked_scales = keep.tile([P, SLOTS], U8, name="picked_scales", align_bytes=64)
+        nc.vector.tensor_copy(picked_scales[:], scale_rows[:, 0:VOCAB].indirect(offsets[:]))
+        for quadrant in range(4):
+            nc.sync.dma_start(out=key_scales[32 * quadrant:32 * quadrant + 4, :].bitcast(I32),
+                              in_=picked_scales[SCALE_BASE + 8 * quadrant:SCALE_BASE + 8 * quadrant + 8, :].bitcast(I32))
+
+        q_raw = keep.tile([P, PASSES, 4, NQ], F32, name="q_raw", tag="shared", align_bytes=64)
+        q_rows = qT[0].rearrange("(o p j) q -> o p j q", o=PASSES, j=4)
+        for o in (EARLY, LATE):
+            nc.sync.dma_start(out=q_raw[:, o, :, :], in_=q_rows[o])
 
         picked_kb = keep.tile([P, SLOTS], F32, name="picked_kb")
         nc.vector.tensor_copy(picked_kb[:], kb_row[:, 0:VOCAB].indirect(offsets[:]))
@@ -76,14 +86,6 @@ def tile_attend_logprob_topk_kernel(tc, qT, k_words, k_scales, kb, ls, offs, out
         for m in range(SLOTS // P):
             nc.tensor.transpose(spread[:, m * P:(m + 1) * P],
                                 kb_cols[:, m:m + 1].to_broadcast([P, P]), ident[:])
-
-        picked_scales = keep.tile([P, SLOTS], U8, name="picked_scales", align_bytes=64)
-        nc.vector.tensor_copy(picked_scales[:], scale_rows[:, 0:VOCAB].indirect(offsets[:]))
-
-        for quadrant in range(4):
-            nc.scalar.dma_start(out=key_scales[32 * quadrant:32 * quadrant + 4, :].bitcast(I32),
-                                in_=picked_scales[96 + 8 * quadrant:96 + 8 * quadrant + 8, :].bitcast(I32))
-
 
         picked_words = keep.tile([P, SLOTS], U32, name="picked_words", align_bytes=64)
         nc.vector.tensor_copy(picked_words[:], words[:].indirect(offsets[:]))
@@ -101,7 +103,7 @@ def tile_attend_logprob_topk_kernel(tc, qT, k_words, k_scales, kb, ls, offs, out
 
         def cast(o, b, copy):
             copy(out=grouped[o, b][:].rearrange("p (c i) t -> p c t i", i=4),
-                 in_=q_raw[o][:, :, b * P:(b + 1) * P].rearrange("p t (c i) -> p c t i", i=4))
+                 in_=q_raw[:, o, :, b * P:(b + 1) * P].rearrange("p t (c i) -> p c t i", i=4))
 
         def quantize(o, b):
             nc.vector.quantize_mx(out=q_codes[o, b][:].bitcast(FP8X4), scales=q_scales[o, b][:],
@@ -117,7 +119,7 @@ def tile_attend_logprob_topk_kernel(tc, qT, k_words, k_scales, kb, ls, offs, out
         cast(LATE, 1, nc.scalar.copy)
         quantize(LATE, 0)
         quantize(LATE, 1)
-        kb_all = keep.tile([P, SLOTS], F32, name="kb_all", tag=f"q_raw{LATE}")
+        kb_all = keep.tile([P, SLOTS], F32, name="kb_all", tag="shared", align_bytes=64)
         nc.scalar.copy(out=kb_all[:], in_=spread[:])
         for o, b in units:
             nc.tensor.matmul_mx(out=acc[b][:], lhsT=q_codes[o, b][:].bitcast(FP8X4), lhsT_scale=q_scales[o, b][:],
@@ -128,6 +130,7 @@ def tile_attend_logprob_topk_kernel(tc, qT, k_words, k_scales, kb, ls, offs, out
             for c in range(0, SLOTS, PIECE):
                 cols = slice(c, c + PIECE)
                 result = keep.tile([P, PIECE], F32, name=f"result{b}_{c}")
-                nc.vector.scalar_tensor_tensor(out=result[:], in0=acc[b][:, cols], scalar=ls_turned[:, P - BLOCKS + b:P - BLOCKS + b + 1],
+                nc.vector.scalar_tensor_tensor(out=result[:], in0=acc[b][:, cols],
+                                               scalar=ls_turned[:, P - BLOCKS + b:P - BLOCKS + b + 1],
                                                in1=kb_all[:, cols], op0=ALU.subtract, op1=ALU.add)
                 nc.sync.dma_start(out=out[0, b * P:(b + 1) * P, cols], in_=result[:])

@@ -21,8 +21,6 @@ KB_ROW = P - 1
 PIECE = 256
 SCALE_ROWS = 16 * PASSES
 SCALE_BASE = 0
-KB_GPSIMD = 2816
-KB_PIECE = 512
 EARLY, LATE = 1, 0
 
 FLOPS = 2 * NQ * SLOTS * D
@@ -34,17 +32,20 @@ def tile_attend_logprob_topk_kernel(tc, qT, k_words, k_scales, kb, ls, offs, out
         keep = ctx.enter_context(tc.tile_pool(name="keep", bufs=1))
         psum = ctx.enter_context(tc.psum_pool(name="psum", bufs=1))
 
+        scale_rows = keep.tile([P, VOCAB], U8, name="scale_rows", tag="shared", align_bytes=64)
+        nc.sync.dma_start(out=scale_rows[0:SCALE_ROWS, :].bitcast(I32),
+                          in_=k_scales.rearrange("o f t -> f o t").bitcast(I32))
+        kb_row = keep.tile([P, VOCAB], F32, name="kb_row", align_bytes=64)
+        nc.sync.dma_start(out=kb_row[KB_ROW:P, :], in_=kb[0:1, :])
         offsets = keep.tile([P, SLOTS // 16], U16, name="offsets")
         nc.sync.dma_start(offsets[:], offs)
-
-        scale_rows = keep.tile([P, VOCAB + 64], U8, name="scale_rows", tag="shared", align_bytes=64)
-        nc.sync.dma_start(out=scale_rows[0:SCALE_ROWS, 0:VOCAB].bitcast(I32),
-                          in_=k_scales.rearrange("o f t -> f o t").bitcast(I32))
-        kb_row = keep.tile([P, VOCAB + 16], F32, name="kb_row", align_bytes=64)
-        nc.sync.dma_start(out=kb_row[KB_ROW:P, 0:VOCAB], in_=kb[0:1, :])
         words = keep.tile([P, VOCAB], U32, name="words", align_bytes=64)
         nc.sync.dma_start(out=words[:].bitcast(I32),
                           in_=k_words[0].rearrange("p t b -> p (t b)").bitcast(I32))
+
+        q_rows = qT[0].rearrange("(o p j) q -> o p j q", o=PASSES, j=4)
+        q_raw = {EARLY: keep.tile([P, 4, NQ], F32, name="q_early")}
+        nc.sync.dma_start(out=q_raw[EARLY][:], in_=q_rows[EARLY])
 
         ls_rows = keep.tile([P, P], F32, name="ls_rows")
         nc.scalar.dma_start(out=ls_rows[P - BLOCKS:P, :], in_=ls[0].rearrange("(b p) o -> b (p o)", p=P))
@@ -52,30 +53,27 @@ def tile_attend_logprob_topk_kernel(tc, qT, k_words, k_scales, kb, ls, offs, out
         ident = keep.tile([P, P], F32, name="ident")
         make_identity(nc, ident[:])
         nc.scalar.copy(ls_rows[0:P - BLOCKS, :], ident[0:P - BLOCKS, :])
-        nc.vector.memset(scale_rows[64:P, 0:VOCAB + 4].bitcast(I32), 0)
-        nc.gpsimd.memset(scale_rows[32:64, 0:VOCAB].bitcast(I32), 0)
+        nc.vector.memset(scale_rows[64:P, :].bitcast(I32), 0)
+        nc.vector.memset(scale_rows[32:64, :].bitcast(I32), 0)
         key_scales = keep.tile([P, PASSES * SLOTS], U8, name="key_scales", align_bytes=64)
         nc.vector.memset(key_scales[:].bitcast(I32), 0)
-        nc.vector.memset(kb_row[0:KB_ROW, KB_GPSIMD:VOCAB + 1], 0.0)
-        for c in range(0, KB_GPSIMD, KB_PIECE):
-            nc.gpsimd.memset(kb_row[0:KB_ROW, c:min(c + KB_PIECE, KB_GPSIMD)], 0.0)
+        nc.vector.memset(kb_row[0:KB_ROW, 0:VOCAB // 2], 0.0)
 
         ls_turned = psum.tile([P, P], F32, name="ls_turned")
         nc.tensor.transpose(ls_turned[:], ls_rows[:], ident[:])
 
         picked_scales = keep.tile([P, SLOTS], U8, name="picked_scales", align_bytes=64)
-        nc.vector.tensor_copy(picked_scales[:], scale_rows[:, 0:VOCAB].indirect(offsets[:]))
+        nc.vector.tensor_copy(picked_scales[:], scale_rows[:].indirect(offsets[:]))
         for quadrant in range(4):
             nc.sync.dma_start(out=key_scales[32 * quadrant:32 * quadrant + 4, :].bitcast(I32),
                               in_=picked_scales[SCALE_BASE + 8 * quadrant:SCALE_BASE + 8 * quadrant + 8, :].bitcast(I32))
 
-        q_raw = keep.tile([P, PASSES, 4, NQ], F32, name="q_raw", tag="shared", align_bytes=64)
-        q_rows = qT[0].rearrange("(o p j) q -> o p j q", o=PASSES, j=4)
-        for o in (EARLY, LATE):
-            nc.sync.dma_start(out=q_raw[:, o, :, :], in_=q_rows[o])
+        q_raw[LATE] = keep.tile([P, 4, NQ], F32, name="q_late", tag="shared", align_bytes=64)
+        nc.sync.dma_start(out=q_raw[LATE][:], in_=q_rows[LATE])
 
+        nc.vector.memset(kb_row[0:KB_ROW, VOCAB // 2:VOCAB], 0.0)
         picked_kb = keep.tile([P, SLOTS], F32, name="picked_kb")
-        nc.vector.tensor_copy(picked_kb[:], kb_row[:, 0:VOCAB].indirect(offsets[:]))
+        nc.vector.tensor_copy(picked_kb[:], kb_row[:].indirect(offsets[:]))
 
         turned = psum.tile([P, SLOTS // P, P], F32, name="turned")
         for m in range(SLOTS // P):
@@ -103,7 +101,7 @@ def tile_attend_logprob_topk_kernel(tc, qT, k_words, k_scales, kb, ls, offs, out
 
         def cast(o, b, copy):
             copy(out=grouped[o, b][:].rearrange("p (c i) t -> p c t i", i=4),
-                 in_=q_raw[:, o, :, b * P:(b + 1) * P].rearrange("p t (c i) -> p c t i", i=4))
+                 in_=q_raw[o][:, :, b * P:(b + 1) * P].rearrange("p t (c i) -> p c t i", i=4))
 
         def quantize(o, b):
             nc.vector.quantize_mx(out=q_codes[o, b][:].bitcast(FP8X4), scales=q_scales[o, b][:],

@@ -94,7 +94,8 @@ def tile_attend_logprob_topk_kernel(tc, qT, k_words, k_scales, kb, ls, offs, out
         grouped = {u: keep.tile([P, P, 4], BF16, name=f"grouped{u[0]}{u[1]}", align_bytes=64) for u in units}
         q_codes = {u: keep.tile([P, P], U32, name=f"q_codes{u[0]}{u[1]}", align_bytes=64) for u in units}
         q_scales = {u: keep.tile([P, P], U8, name=f"q_scales{u[0]}{u[1]}", align_bytes=64) for u in units}
-        acc = [psum.tile([P, SLOTS], F32, name=f"acc{b}") for b in range(BLOCKS)]
+        acc = {(b, c): psum.tile([P, PIECE], F32, name=f"acc{b}_{c}")
+               for b in range(BLOCKS) for c in range(0, SLOTS, PIECE)}
 
         def part(o):
             nc.vector.tensor_copy(key_codes[o][:], halves[:, o, :])
@@ -120,15 +121,18 @@ def tile_attend_logprob_topk_kernel(tc, qT, k_words, k_scales, kb, ls, offs, out
         kb_all = keep.tile([P, SLOTS], F32, name="kb_all", tag="shared", align_bytes=64)
         nc.scalar.copy(out=kb_all[:], in_=spread[:])
         for o, b in units:
-            nc.tensor.matmul_mx(out=acc[b][:], lhsT=q_codes[o, b][:].bitcast(FP8X4), lhsT_scale=q_scales[o, b][:],
-                                rhs=key_codes[o][:].bitcast(FP4X4),
-                                rhs_scale=key_scales[:, o * SLOTS:(o + 1) * SLOTS],
-                                start=(o == EARLY), stop=(o == LATE))
+            for n in range(0, SLOTS, P):
+                c, at = n - n % PIECE, n % PIECE
+                nc.tensor.matmul_mx(out=acc[b, c][:, at:at + P], lhsT=q_codes[o, b][:].bitcast(FP8X4),
+                                    lhsT_scale=q_scales[o, b][:],
+                                    rhs=key_codes[o][:, n:n + P].bitcast(FP4X4),
+                                    rhs_scale=key_scales[:, o * SLOTS + n:o * SLOTS + n + P],
+                                    start=(o == EARLY and at == 0), stop=(o == LATE and at + P == PIECE))
         for b in range(BLOCKS):
             for c in range(0, SLOTS, PIECE):
                 cols = slice(c, c + PIECE)
                 result = keep.tile([P, PIECE], F32, name=f"result{b}_{c}")
-                nc.vector.scalar_tensor_tensor(out=result[:], in0=acc[b][:, cols],
+                nc.vector.scalar_tensor_tensor(out=result[:], in0=acc[b, c][:],
                                                scalar=ls_turned[:, P - BLOCKS + b:P - BLOCKS + b + 1],
                                                in1=kb_all[:, cols], op0=ALU.subtract, op1=ALU.add)
                 nc.sync.dma_start(out=out[0, b * P:(b + 1) * P, cols], in_=result[:])

@@ -36,7 +36,7 @@ def tile_attend_logprob_topk_kernel(tc, qT, k_words, k_scales, kb, ls, offs, out
         nc.sync.dma_start(out=scale_rows[0:SCALE_ROWS, :].bitcast(I32),
                           in_=k_scales.rearrange("o f t -> f o t").bitcast(I32))
         kb_row = keep.tile([P, VOCAB], F32, name="kb_row", align_bytes=64)
-        nc.sync.dma_start(out=kb_row[KB_ROW:P, :], in_=kb[0:1, :])
+        nc.scalar.dma_start(out=kb_row[KB_ROW:P, :], in_=kb[0:1, :])
         offsets = keep.tile([P, SLOTS // 16], U16, name="offsets")
         nc.sync.dma_start(offsets[:], offs)
         words = keep.tile([P, VOCAB], U32, name="words", align_bytes=64)
@@ -57,7 +57,7 @@ def tile_attend_logprob_topk_kernel(tc, qT, k_words, k_scales, kb, ls, offs, out
         nc.vector.memset(scale_rows[32:64, :].bitcast(I32), 0)
         key_scales = keep.tile([P, PASSES * SLOTS], U8, name="key_scales", align_bytes=64)
         nc.vector.memset(key_scales[:].bitcast(I32), 0)
-        nc.vector.memset(kb_row[0:KB_ROW, 0:VOCAB // 2], 0.0)
+        nc.vector.memset(kb_row[0:KB_ROW, :], 0.0)
 
         ls_turned = psum.tile([P, P], F32, name="ls_turned")
         nc.tensor.transpose(ls_turned[:], ls_rows[:], ident[:])
@@ -71,7 +71,6 @@ def tile_attend_logprob_topk_kernel(tc, qT, k_words, k_scales, kb, ls, offs, out
         q_raw[LATE] = keep.tile([P, 4, NQ], F32, name="q_late", tag="shared", align_bytes=64)
         nc.sync.dma_start(out=q_raw[LATE][:], in_=q_rows[LATE])
 
-        nc.vector.memset(kb_row[0:KB_ROW, VOCAB // 2:VOCAB], 0.0)
         picked_kb = keep.tile([P, SLOTS], F32, name="picked_kb")
         nc.vector.tensor_copy(picked_kb[:], kb_row[:].indirect(offsets[:]))
 

@@ -19,6 +19,8 @@ PASSES = D // 512
 BLOCKS = NQ // P
 KB_ROW = P - 1
 PIECE = 256
+VECTOR_SHARE = 48
+SCALAR_SHARES = (48, 64)
 SCALE_ROWS = 16 * PASSES
 SCALE_BASE = 0
 EARLY, LATE = 1, 0
@@ -44,11 +46,11 @@ def tile_attend_logprob_topk_kernel(tc, qT, k_words, k_scales, kb, ls, offs, out
                           in_=k_words[0].rearrange("p t b -> p (t b)").bitcast(I32))
 
         q_rows = qT[0].rearrange("(o p j) q -> o p j q", o=PASSES, j=4)
-        q_raw = {EARLY: keep.tile([P, 4, NQ], F32, name="q_early")}
+        q_raw = {EARLY: keep.tile([P, 4, NQ], F32, name="q_early", tag="early_then_kb")}
         nc.sync.dma_start(out=q_raw[EARLY][:], in_=q_rows[EARLY])
 
-        ls_rows = keep.tile([P, P], F32, name="ls_rows")
-        nc.scalar.dma_start(out=ls_rows[P - BLOCKS:P, :], in_=ls[0].rearrange("(b p) o -> b (p o)", p=P))
+        ls_rows = keep.tile([P, P], F32, name="ls_rows", tag="ls_then_late_codes", align_bytes=64)
+        nc.sync.dma_start(out=ls_rows[P - BLOCKS:P, :], in_=ls[0].rearrange("(b p) o -> b (p o)", p=P))
 
         ident = keep.tile([P, P], F32, name="ident")
         make_identity(nc, ident[:])
@@ -87,7 +89,8 @@ def tile_attend_logprob_topk_kernel(tc, qT, k_words, k_scales, kb, ls, offs, out
         picked_words = keep.tile([P, SLOTS], U32, name="picked_words", align_bytes=64)
         nc.vector.tensor_copy(picked_words[:], words[:].indirect(offsets[:]))
         halves = picked_words[:].bitcast(U16).rearrange("p (n h) -> p h n", h=2)
-        key_codes = [keep.tile([P, SLOTS], U16, name=f"key_codes{o}", align_bytes=64) for o in range(PASSES)]
+        key_codes = {EARLY: keep.tile([P, SLOTS], U16, name="early_codes", align_bytes=64),
+                     LATE: keep.tile([P, SLOTS], U16, name="late_codes", tag="ls_then_late_codes", align_bytes=64)}
 
         units = [(o, b) for o in (EARLY, LATE) for b in range(BLOCKS)]
         grouped = {u: keep.tile([P, P, 4], BF16, name=f"grouped{u[0]}{u[1]}", align_bytes=64) for u in units}
@@ -99,9 +102,9 @@ def tile_attend_logprob_topk_kernel(tc, qT, k_words, k_scales, kb, ls, offs, out
         def part(o):
             nc.vector.tensor_copy(key_codes[o][:], halves[:, o, :])
 
-        def cast(o, b, copy):
-            copy(out=grouped[o, b][:].rearrange("p (c i) t -> p c t i", i=4),
-                 in_=q_raw[o][:, :, b * P:(b + 1) * P].rearrange("p t (c i) -> p c t i", i=4))
+        def cast(o, b, copy, lo=0, hi=P):
+            copy(out=grouped[o, b][:, lo:hi, :].rearrange("p (c i) t -> p c t i", i=4),
+                 in_=q_raw[o][:, :, b * P + lo:b * P + hi].rearrange("p t (c i) -> p c t i", i=4))
 
         def quantize(o, b):
             nc.vector.quantize_mx(out=q_codes[o, b][:].bitcast(FP8X4), scales=q_scales[o, b][:],
@@ -109,16 +112,20 @@ def tile_attend_logprob_topk_kernel(tc, qT, k_words, k_scales, kb, ls, offs, out
 
         part(EARLY)
         cast(EARLY, 0, nc.scalar.copy)
-        cast(EARLY, 1, nc.scalar.copy)
+        cast(EARLY, 1, nc.vector.tensor_copy, 0, VECTOR_SHARE)
+        cast(EARLY, 1, nc.scalar.copy, VECTOR_SHARE, P)
         quantize(EARLY, 0)
         part(LATE)
         quantize(EARLY, 1)
-        cast(LATE, 0, nc.vector.tensor_copy)
-        cast(LATE, 1, nc.scalar.copy)
+        kb_all = {0: keep.tile([P, PIECE], F32, name="kb_first", tag="early_then_kb")}
+        nc.scalar.copy(out=kb_all[0][:], in_=spread[:, 0:PIECE])
+        for b, share in enumerate(SCALAR_SHARES):
+            cast(LATE, b, nc.vector.tensor_copy, 0, P - share)
+            cast(LATE, b, nc.scalar.copy, P - share, P)
         quantize(LATE, 0)
         quantize(LATE, 1)
-        kb_all = keep.tile([P, SLOTS], F32, name="kb_all", tag="shared", align_bytes=64)
-        nc.scalar.copy(out=kb_all[:], in_=spread[:])
+        kb_all[PIECE] = keep.tile([P, PIECE], F32, name="kb_second", tag="shared", align_bytes=64)
+        nc.scalar.copy(out=kb_all[PIECE][:], in_=spread[:, PIECE:SLOTS])
         for o, b in units:
             for n in range(0, SLOTS, P):
                 c, at = n - n % PIECE, n % PIECE
@@ -133,5 +140,5 @@ def tile_attend_logprob_topk_kernel(tc, qT, k_words, k_scales, kb, ls, offs, out
                 result = keep.tile([P, PIECE], F32, name=f"result{b}_{c}")
                 nc.vector.scalar_tensor_tensor(out=result[:], in0=acc[b, c][:],
                                                scalar=ls_turned[:, P - BLOCKS + b:P - BLOCKS + b + 1],
-                                               in1=kb_all[:, cols], op0=ALU.subtract, op1=ALU.add)
+                                               in1=kb_all[c][:], op0=ALU.subtract, op1=ALU.add)
                 nc.sync.dma_start(out=out[0, b * P:(b + 1) * P, cols], in_=result[:])

@@ -12,6 +12,7 @@ U8 = mybir.dt.uint8
 FP8X4 = mybir.dt.float8_e4m3fn_x4
 FP4X4 = mybir.dt.float4_e2m1fn_x4
 ALU = mybir.AluOpType
+COPY = mybir.ActivationFunctionType.Copy
 
 P = 128
 SLOTS, VOCAB, D, NQ = 512, 4096, 1024, 256
@@ -19,10 +20,8 @@ PASSES = D // 512
 BLOCKS = NQ // P
 KB_ROW = P - 1
 PIECE = 256
-VECTOR_SHARE = 48
 SCALAR_SHARES = (48, 64)
 SCALE_ROWS = 16 * PASSES
-SCALE_BASE = 0
 EARLY, LATE = 1, 0
 
 FLOPS = 2 * NQ * SLOTS * D
@@ -38,44 +37,33 @@ def tile_attend_logprob_topk_kernel(tc, qT, k_words, k_scales, kb, ls, offs, out
         nc.sync.dma_start(out=scale_rows[0:SCALE_ROWS, :].bitcast(I32),
                           in_=k_scales.rearrange("o f t -> f o t").bitcast(I32))
         kb_row = keep.tile([P, VOCAB], F32, name="kb_row", align_bytes=64)
-        nc.scalar.dma_start(out=kb_row[KB_ROW:P, :], in_=kb[0:1, :])
+        nc.sync.dma_start(out=kb_row[KB_ROW:P, :], in_=kb[0:1, :])
         offsets = keep.tile([P, SLOTS // 16], U16, name="offsets")
         nc.sync.dma_start(offsets[:], offs)
+        ls_rows = keep.tile([P, P], F32, name="ls_rows", align_bytes=64)
+        nc.scalar.dma_start(out=ls_rows[P - BLOCKS:P, :], in_=ls[0].rearrange("(b p) o -> b (p o)", p=P))
         words = keep.tile([P, VOCAB], U32, name="words", align_bytes=64)
         nc.sync.dma_start(out=words[:].bitcast(I32),
                           in_=k_words[0].rearrange("p t b -> p (t b)").bitcast(I32))
 
         q_rows = qT[0].rearrange("(o p j) q -> o p j q", o=PASSES, j=4)
-        q_raw = {EARLY: keep.tile([P, 4, NQ], F32, name="q_early", tag="early_then_kb")}
+        q_raw = {EARLY: keep.tile([P, 4, NQ], F32, name="q_early")}
         nc.sync.dma_start(out=q_raw[EARLY][:], in_=q_rows[EARLY])
-
-        ls_rows = keep.tile([P, P], F32, name="ls_rows", tag="ls_then_late_codes", align_bytes=64)
-        nc.sync.dma_start(out=ls_rows[P - BLOCKS:P, :], in_=ls[0].rearrange("(b p) o -> b (p o)", p=P))
 
         ident = keep.tile([P, P], F32, name="ident")
         make_identity(nc, ident[:])
         nc.scalar.copy(ls_rows[0:P - BLOCKS, :], ident[0:P - BLOCKS, :])
+        nc.vector.memset(kb_row[0:KB_ROW, :], 0.0)
         nc.vector.memset(scale_rows[64:P, :].bitcast(I32), 0)
         nc.vector.memset(scale_rows[32:64, :].bitcast(I32), 0)
         key_scales = keep.tile([P, PASSES * SLOTS], U8, name="key_scales", align_bytes=64)
         nc.vector.memset(key_scales[:].bitcast(I32), 0)
-        nc.vector.memset(kb_row[0:KB_ROW, :], 0.0)
 
         ls_turned = psum.tile([P, P], F32, name="ls_turned")
         nc.tensor.transpose(ls_turned[:], ls_rows[:], ident[:])
 
-        picked_scales = keep.tile([P, SLOTS], U8, name="picked_scales", align_bytes=64)
-        nc.vector.tensor_copy(picked_scales[:], scale_rows[:].indirect(offsets[:]))
-        for quadrant in range(4):
-            nc.sync.dma_start(out=key_scales[32 * quadrant:32 * quadrant + 4, :].bitcast(I32),
-                              in_=picked_scales[SCALE_BASE + 8 * quadrant:SCALE_BASE + 8 * quadrant + 8, :].bitcast(I32))
-
-        q_raw[LATE] = keep.tile([P, 4, NQ], F32, name="q_late", tag="shared", align_bytes=64)
-        nc.sync.dma_start(out=q_raw[LATE][:], in_=q_rows[LATE])
-
         picked_kb = keep.tile([P, SLOTS], F32, name="picked_kb")
-        nc.vector.tensor_copy(picked_kb[:], kb_row[:].indirect(offsets[:]))
-
+        nc.scalar.activation(picked_kb[:], kb_row[:].indirect(offsets[:]), COPY)
         turned = psum.tile([P, SLOTS // P, P], F32, name="turned")
         for m in range(SLOTS // P):
             nc.tensor.transpose(turned[:, m, :], picked_kb[:, m * P:(m + 1) * P], ident[:])
@@ -85,12 +73,22 @@ def tile_attend_logprob_topk_kernel(tc, qT, k_words, k_scales, kb, ls, offs, out
         for m in range(SLOTS // P):
             nc.tensor.transpose(spread[:, m * P:(m + 1) * P],
                                 kb_cols[:, m:m + 1].to_broadcast([P, P]), ident[:])
+        kb_all = keep.tile([P, SLOTS], F32, name="kb_all")
+        nc.scalar.copy(out=kb_all[:], in_=spread[:])
+
+        picked_scales = keep.tile([P, SLOTS], U8, name="picked_scales", align_bytes=64)
+        nc.vector.tensor_copy(picked_scales[:], scale_rows[:].indirect(offsets[:]))
+        for quadrant in range(4):
+            nc.sync.dma_start(out=key_scales[32 * quadrant:32 * quadrant + 4, :].bitcast(I32),
+                              in_=picked_scales[8 * quadrant:8 * quadrant + 8, :].bitcast(I32))
+
+        q_raw[LATE] = keep.tile([P, 4, NQ], F32, name="q_late", tag="shared", align_bytes=64)
+        nc.sync.dma_start(out=q_raw[LATE][:], in_=q_rows[LATE])
 
         picked_words = keep.tile([P, SLOTS], U32, name="picked_words", align_bytes=64)
         nc.vector.tensor_copy(picked_words[:], words[:].indirect(offsets[:]))
         halves = picked_words[:].bitcast(U16).rearrange("p (n h) -> p h n", h=2)
-        key_codes = {EARLY: keep.tile([P, SLOTS], U16, name="early_codes", align_bytes=64),
-                     LATE: keep.tile([P, SLOTS], U16, name="late_codes", tag="ls_then_late_codes", align_bytes=64)}
+        key_codes = {o: keep.tile([P, SLOTS], U16, name=f"key_codes{o}", align_bytes=64) for o in (EARLY, LATE)}
 
         units = [(o, b) for o in (EARLY, LATE) for b in range(BLOCKS)]
         grouped = {u: keep.tile([P, P, 4], BF16, name=f"grouped{u[0]}{u[1]}", align_bytes=64) for u in units}
@@ -98,9 +96,6 @@ def tile_attend_logprob_topk_kernel(tc, qT, k_words, k_scales, kb, ls, offs, out
         q_scales = {u: keep.tile([P, P], U8, name=f"q_scales{u[0]}{u[1]}", align_bytes=64) for u in units}
         acc = {(b, c): psum.tile([P, PIECE], F32, name=f"acc{b}_{c}")
                for b in range(BLOCKS) for c in range(0, SLOTS, PIECE)}
-
-        def part(o):
-            nc.vector.tensor_copy(key_codes[o][:], halves[:, o, :])
 
         def cast(o, b, copy, lo=0, hi=P):
             copy(out=grouped[o, b][:, lo:hi, :].rearrange("p (c i) t -> p c t i", i=4),
@@ -110,22 +105,16 @@ def tile_attend_logprob_topk_kernel(tc, qT, k_words, k_scales, kb, ls, offs, out
             nc.vector.quantize_mx(out=q_codes[o, b][:].bitcast(FP8X4), scales=q_scales[o, b][:],
                                   in_=grouped[o, b][:].rearrange("p w t -> p (w t)"))
 
-        part(EARLY)
-        cast(EARLY, 0, nc.scalar.copy)
-        cast(EARLY, 1, nc.vector.tensor_copy, 0, VECTOR_SHARE)
-        cast(EARLY, 1, nc.scalar.copy, VECTOR_SHARE, P)
-        quantize(EARLY, 0)
-        part(LATE)
-        quantize(EARLY, 1)
-        kb_all = {0: keep.tile([P, PIECE], F32, name="kb_first", tag="early_then_kb")}
-        nc.scalar.copy(out=kb_all[0][:], in_=spread[:, 0:PIECE])
+        for o in (EARLY, LATE):
+            nc.vector.tensor_copy(key_codes[o][:], halves[:, o, :])
+        for b in range(BLOCKS):
+            cast(EARLY, b, nc.scalar.copy)
+            quantize(EARLY, b)
         for b, share in enumerate(SCALAR_SHARES):
             cast(LATE, b, nc.vector.tensor_copy, 0, P - share)
             cast(LATE, b, nc.scalar.copy, P - share, P)
-        quantize(LATE, 0)
-        quantize(LATE, 1)
-        kb_all[PIECE] = keep.tile([P, PIECE], F32, name="kb_second", tag="shared", align_bytes=64)
-        nc.scalar.copy(out=kb_all[PIECE][:], in_=spread[:, PIECE:SLOTS])
+        for b in range(BLOCKS):
+            quantize(LATE, b)
         for o, b in units:
             for n in range(0, SLOTS, P):
                 c, at = n - n % PIECE, n % PIECE
@@ -140,5 +129,5 @@ def tile_attend_logprob_topk_kernel(tc, qT, k_words, k_scales, kb, ls, offs, out
                 result = keep.tile([P, PIECE], F32, name=f"result{b}_{c}")
                 nc.vector.scalar_tensor_tensor(out=result[:], in0=acc[b, c][:],
                                                scalar=ls_turned[:, P - BLOCKS + b:P - BLOCKS + b + 1],
-                                               in1=kb_all[c][:], op0=ALU.subtract, op1=ALU.add)
+                                               in1=kb_all[:, cols], op0=ALU.subtract, op1=ALU.add)
                 nc.sync.dma_start(out=out[0, b * P:(b + 1) * P, cols], in_=result[:])

@@ -20,6 +20,7 @@ PASSES = D // 512
 BLOCKS = NQ // P
 KB_ROW = P - 1
 PIECE = 256
+FIRST_SHARE = 56
 SCALAR_SHARES = (48, 64)
 SCALE_ROWS = 16 * PASSES
 EARLY, LATE = 1, 0
@@ -40,8 +41,6 @@ def tile_attend_logprob_topk_kernel(tc, qT, k_words, k_scales, kb, ls, offs, out
         nc.sync.dma_start(out=kb_row[KB_ROW:P, :], in_=kb[0:1, :])
         offsets = keep.tile([P, SLOTS // 16], U16, name="offsets")
         nc.sync.dma_start(offsets[:], offs)
-        ls_rows = keep.tile([P, P], F32, name="ls_rows", align_bytes=64)
-        nc.scalar.dma_start(out=ls_rows[P - BLOCKS:P, :], in_=ls[0].rearrange("(b p) o -> b (p o)", p=P))
         words = keep.tile([P, VOCAB], U32, name="words", align_bytes=64)
         nc.sync.dma_start(out=words[:].bitcast(I32),
                           in_=k_words[0].rearrange("p t b -> p (t b)").bitcast(I32))
@@ -49,6 +48,9 @@ def tile_attend_logprob_topk_kernel(tc, qT, k_words, k_scales, kb, ls, offs, out
         q_rows = qT[0].rearrange("(o p j) q -> o p j q", o=PASSES, j=4)
         q_raw = {EARLY: keep.tile([P, 4, NQ], F32, name="q_early")}
         nc.sync.dma_start(out=q_raw[EARLY][:], in_=q_rows[EARLY])
+
+        ls_rows = keep.tile([P, P], F32, name="ls_rows", tag="ls_then_codes", align_bytes=64)
+        nc.sync.dma_start(out=ls_rows[P - BLOCKS:P, :], in_=ls[0].rearrange("(b p) o -> b (p o)", p=P))
 
         ident = keep.tile([P, P], F32, name="ident")
         make_identity(nc, ident[:])
@@ -86,9 +88,14 @@ def tile_attend_logprob_topk_kernel(tc, qT, k_words, k_scales, kb, ls, offs, out
         nc.sync.dma_start(out=q_raw[LATE][:], in_=q_rows[LATE])
 
         picked_words = keep.tile([P, SLOTS], U32, name="picked_words", align_bytes=64)
-        nc.vector.tensor_copy(picked_words[:], words[:].indirect(offsets[:]))
+        for c in range(0, SLOTS, PIECE):
+            nc.vector.tensor_copy(picked_words[:, c:c + PIECE],
+                                  words[:].indirect(offsets[:, c // 16:(c + PIECE) // 16]))
         halves = picked_words[:].bitcast(U16).rearrange("p (n h) -> p h n", h=2)
-        key_codes = {o: keep.tile([P, SLOTS], U16, name=f"key_codes{o}", align_bytes=64) for o in (EARLY, LATE)}
+        first_codes = keep.tile([P, PIECE], U16, name="first_codes", align_bytes=64)
+        other_codes = keep.tile([P, PIECE + SLOTS], U16, name="other_codes", tag="ls_then_codes", align_bytes=64)
+        key_codes = {(EARLY, 0): first_codes[:], (EARLY, PIECE): other_codes[:, 0:PIECE],
+                     (LATE, 0): other_codes[:, PIECE:SLOTS], (LATE, PIECE): other_codes[:, SLOTS:SLOTS + PIECE]}
 
         units = [(o, b) for o in (EARLY, LATE) for b in range(BLOCKS)]
         grouped = {u: keep.tile([P, P, 4], BF16, name=f"grouped{u[0]}{u[1]}", align_bytes=64) for u in units}
@@ -105,11 +112,14 @@ def tile_attend_logprob_topk_kernel(tc, qT, k_words, k_scales, kb, ls, offs, out
             nc.vector.quantize_mx(out=q_codes[o, b][:].bitcast(FP8X4), scales=q_scales[o, b][:],
                                   in_=grouped[o, b][:].rearrange("p w t -> p (w t)"))
 
-        for o in (EARLY, LATE):
-            nc.vector.tensor_copy(key_codes[o][:], halves[:, o, :])
-        for b in range(BLOCKS):
-            cast(EARLY, b, nc.scalar.copy)
-            quantize(EARLY, b)
+        nc.vector.tensor_copy(first_codes[:], halves[:, EARLY, 0:PIECE])
+        cast(EARLY, 0, nc.vector.tensor_copy, 0, FIRST_SHARE)
+        cast(EARLY, 0, nc.scalar.copy, FIRST_SHARE, P)
+        quantize(EARLY, 0)
+        nc.vector.tensor_copy(other_codes[:, 0:PIECE], halves[:, EARLY, PIECE:SLOTS])
+        nc.vector.tensor_copy(other_codes[:, PIECE:PIECE + SLOTS], halves[:, LATE, :])
+        cast(EARLY, 1, nc.scalar.copy)
+        quantize(EARLY, 1)
         for b, share in enumerate(SCALAR_SHARES):
             cast(LATE, b, nc.vector.tensor_copy, 0, P - share)
             cast(LATE, b, nc.scalar.copy, P - share, P)
@@ -120,7 +130,7 @@ def tile_attend_logprob_topk_kernel(tc, qT, k_words, k_scales, kb, ls, offs, out
                 c, at = n - n % PIECE, n % PIECE
                 nc.tensor.matmul_mx(out=acc[b, c][:, at:at + P], lhsT=q_codes[o, b][:].bitcast(FP8X4),
                                     lhsT_scale=q_scales[o, b][:],
-                                    rhs=key_codes[o][:, n:n + P].bitcast(FP4X4),
+                                    rhs=key_codes[o, c][:, at:at + P].bitcast(FP4X4),
                                     rhs_scale=key_scales[:, o * SLOTS + n:o * SLOTS + n + P],
                                     start=(o == EARLY and at == 0), stop=(o == LATE and at + P == PIECE))
         for b in range(BLOCKS):

@@ -19,9 +19,10 @@ SLOTS, VOCAB, D, NQ = 512, 4096, 1024, 256
 PASSES = D // 512
 BLOCKS = NQ // P
 KB_ROW = P - 1
-PIECE = 256
+HALF = SLOTS // 2
+PIECES = ((128, 128, 256), (256, 256))
 FIRST_SHARE = 56
-SCALAR_SHARES = (48, 64)
+LATE_SHARES = (56, 96)
 SCALE_ROWS = 16 * PASSES
 EARLY, LATE = 1, 0
 
@@ -34,9 +35,9 @@ def tile_attend_logprob_topk_kernel(tc, qT, k_words, k_scales, kb, ls, offs, out
         keep = ctx.enter_context(tc.tile_pool(name="keep", bufs=1))
         psum = ctx.enter_context(tc.psum_pool(name="psum", bufs=1))
 
-        scale_rows = keep.tile([P, VOCAB], U8, name="scale_rows", tag="shared", align_bytes=64)
+        scale_rows = keep.tile([P, VOCAB], U8, name="scale_rows", align_bytes=64)
         nc.sync.dma_start(out=scale_rows[0:SCALE_ROWS, :].bitcast(I32),
-                          in_=k_scales.rearrange("o f t -> f o t").bitcast(I32))
+                          in_=k_scales.rearrange("o f t -> (o f) t").bitcast(I32))
         kb_row = keep.tile([P, VOCAB], F32, name="kb_row", align_bytes=64)
         nc.sync.dma_start(out=kb_row[KB_ROW:P, :], in_=kb[0:1, :])
         offsets = keep.tile([P, SLOTS // 16], U16, name="offsets")
@@ -45,24 +46,33 @@ def tile_attend_logprob_topk_kernel(tc, qT, k_words, k_scales, kb, ls, offs, out
         nc.sync.dma_start(out=words[:].bitcast(I32),
                           in_=k_words[0].rearrange("p t b -> p (t b)").bitcast(I32))
 
-        q_rows = qT[0].rearrange("(o p j) q -> o p j q", o=PASSES, j=4)
-        q_raw = {EARLY: keep.tile([P, 4, NQ], F32, name="q_early")}
-        nc.sync.dma_start(out=q_raw[EARLY][:], in_=q_rows[EARLY])
-
-        ls_rows = keep.tile([P, P], F32, name="ls_rows", tag="ls_then_codes", align_bytes=64)
-        nc.sync.dma_start(out=ls_rows[P - BLOCKS:P, :], in_=ls[0].rearrange("(b p) o -> b (p o)", p=P))
-
         ident = keep.tile([P, P], F32, name="ident")
         make_identity(nc, ident[:])
+        ls_rows = keep.tile([P, P], F32, name="ls_rows", tag="ls_then_codes", align_bytes=64)
         nc.scalar.copy(ls_rows[0:P - BLOCKS, :], ident[0:P - BLOCKS, :])
+
         nc.vector.memset(kb_row[0:KB_ROW, :], 0.0)
         nc.vector.memset(scale_rows[64:P, :].bitcast(I32), 0)
         nc.vector.memset(scale_rows[32:64, :].bitcast(I32), 0)
         key_scales = keep.tile([P, PASSES * SLOTS], U8, name="key_scales", align_bytes=64)
         nc.vector.memset(key_scales[:].bitcast(I32), 0)
+        picked_scales = keep.tile([P, SLOTS], U8, name="picked_scales", align_bytes=64)
+        nc.vector.tensor_copy(picked_scales[:], scale_rows[:].indirect(offsets[:]))
 
-        ls_turned = psum.tile([P, P], F32, name="ls_turned")
-        nc.tensor.transpose(ls_turned[:], ls_rows[:], ident[:])
+        def move_scales(o):
+            for quadrant in range(4):
+                first = 16 * o + 4 * quadrant
+                nc.sync.dma_start(
+                    out=key_scales[32 * quadrant:32 * quadrant + 4, o * SLOTS:(o + 1) * SLOTS].bitcast(I32),
+                    in_=picked_scales[first:first + 4, :].bitcast(I32))
+
+        q_rows = qT[0].rearrange("(o p j) q -> o p j q", o=PASSES, j=4)
+        q_raw = {o: keep.tile([P, 4, NQ], F32, name=f"q_raw{o}") for o in (EARLY, LATE)}
+        nc.sync.dma_start(out=q_raw[EARLY][:], in_=q_rows[EARLY])
+        nc.sync.dma_start(out=ls_rows[P - BLOCKS:P, :], in_=ls[0].rearrange("(b p) o -> b (p o)", p=P))
+        move_scales(EARLY)
+        nc.sync.dma_start(out=q_raw[LATE][:], in_=q_rows[LATE])
+        move_scales(LATE)
 
         picked_kb = keep.tile([P, SLOTS], F32, name="picked_kb")
         nc.scalar.activation(picked_kb[:], kb_row[:].indirect(offsets[:]), COPY)
@@ -77,32 +87,25 @@ def tile_attend_logprob_topk_kernel(tc, qT, k_words, k_scales, kb, ls, offs, out
                                 kb_cols[:, m:m + 1].to_broadcast([P, P]), ident[:])
         kb_all = keep.tile([P, SLOTS], F32, name="kb_all")
         nc.scalar.copy(out=kb_all[:], in_=spread[:])
-
-        picked_scales = keep.tile([P, SLOTS], U8, name="picked_scales", align_bytes=64)
-        nc.vector.tensor_copy(picked_scales[:], scale_rows[:].indirect(offsets[:]))
-        for quadrant in range(4):
-            nc.sync.dma_start(out=key_scales[32 * quadrant:32 * quadrant + 4, :].bitcast(I32),
-                              in_=picked_scales[8 * quadrant:8 * quadrant + 8, :].bitcast(I32))
-
-        q_raw[LATE] = keep.tile([P, 4, NQ], F32, name="q_late", tag="shared", align_bytes=64)
-        nc.sync.dma_start(out=q_raw[LATE][:], in_=q_rows[LATE])
+        ls_turned = psum.tile([P, P], F32, name="ls_turned")
+        nc.tensor.transpose(ls_turned[:], ls_rows[:], ident[:])
 
         picked_words = keep.tile([P, SLOTS], U32, name="picked_words", align_bytes=64)
-        for c in range(0, SLOTS, PIECE):
-            nc.vector.tensor_copy(picked_words[:, c:c + PIECE],
-                                  words[:].indirect(offsets[:, c // 16:(c + PIECE) // 16]))
+        for c in (0, HALF):
+            nc.vector.tensor_copy(picked_words[:, c:c + HALF],
+                                  words[:].indirect(offsets[:, c // 16:(c + HALF) // 16]))
         halves = picked_words[:].bitcast(U16).rearrange("p (n h) -> p h n", h=2)
-        first_codes = keep.tile([P, PIECE], U16, name="first_codes", align_bytes=64)
-        other_codes = keep.tile([P, PIECE + SLOTS], U16, name="other_codes", tag="ls_then_codes", align_bytes=64)
-        key_codes = {(EARLY, 0): first_codes[:], (EARLY, PIECE): other_codes[:, 0:PIECE],
-                     (LATE, 0): other_codes[:, PIECE:SLOTS], (LATE, PIECE): other_codes[:, SLOTS:SLOTS + PIECE]}
+        first_codes = keep.tile([P, HALF], U16, name="first_codes", align_bytes=64)
+        other_codes = keep.tile([P, HALF + SLOTS], U16, name="other_codes", tag="ls_then_codes", align_bytes=64)
+        key_codes = {(EARLY, 0): first_codes[:], (EARLY, HALF): other_codes[:, 0:HALF],
+                     (LATE, 0): other_codes[:, HALF:SLOTS], (LATE, HALF): other_codes[:, SLOTS:SLOTS + HALF]}
 
         units = [(o, b) for o in (EARLY, LATE) for b in range(BLOCKS)]
         grouped = {u: keep.tile([P, P, 4], BF16, name=f"grouped{u[0]}{u[1]}", align_bytes=64) for u in units}
         q_codes = {u: keep.tile([P, P], U32, name=f"q_codes{u[0]}{u[1]}", align_bytes=64) for u in units}
         q_scales = {u: keep.tile([P, P], U8, name=f"q_scales{u[0]}{u[1]}", align_bytes=64) for u in units}
-        acc = {(b, c): psum.tile([P, PIECE], F32, name=f"acc{b}_{c}")
-               for b in range(BLOCKS) for c in range(0, SLOTS, PIECE)}
+        pieces = [(b, sum(widths[:k]), w) for b, widths in enumerate(PIECES) for k, w in enumerate(widths)]
+        acc = {(b, c): psum.tile([P, w], F32, name=f"acc{b}_{c}") for b, c, w in pieces}
 
         def cast(o, b, copy, lo=0, hi=P):
             copy(out=grouped[o, b][:, lo:hi, :].rearrange("p (c i) t -> p c t i", i=4),
@@ -112,32 +115,30 @@ def tile_attend_logprob_topk_kernel(tc, qT, k_words, k_scales, kb, ls, offs, out
             nc.vector.quantize_mx(out=q_codes[o, b][:].bitcast(FP8X4), scales=q_scales[o, b][:],
                                   in_=grouped[o, b][:].rearrange("p w t -> p (w t)"))
 
-        nc.vector.tensor_copy(first_codes[:], halves[:, EARLY, 0:PIECE])
+        nc.vector.tensor_copy(first_codes[:], halves[:, EARLY, 0:HALF])
         cast(EARLY, 0, nc.vector.tensor_copy, 0, FIRST_SHARE)
         cast(EARLY, 0, nc.scalar.copy, FIRST_SHARE, P)
         quantize(EARLY, 0)
-        nc.vector.tensor_copy(other_codes[:, 0:PIECE], halves[:, EARLY, PIECE:SLOTS])
-        nc.vector.tensor_copy(other_codes[:, PIECE:PIECE + SLOTS], halves[:, LATE, :])
+        nc.vector.tensor_copy(other_codes[:, 0:HALF], halves[:, EARLY, HALF:SLOTS])
+        nc.vector.tensor_copy(other_codes[:, HALF:HALF + SLOTS], halves[:, LATE, :])
         cast(EARLY, 1, nc.scalar.copy)
         quantize(EARLY, 1)
-        for b, share in enumerate(SCALAR_SHARES):
-            cast(LATE, b, nc.vector.tensor_copy, 0, P - share)
-            cast(LATE, b, nc.scalar.copy, P - share, P)
+        for b, share in enumerate(LATE_SHARES):
+            cast(LATE, b, nc.vector.tensor_copy, 0, share)
+            cast(LATE, b, nc.scalar.copy, share, P)
         for b in range(BLOCKS):
             quantize(LATE, b)
-        for o, b in units:
-            for n in range(0, SLOTS, P):
-                c, at = n - n % PIECE, n % PIECE
-                nc.tensor.matmul_mx(out=acc[b, c][:, at:at + P], lhsT=q_codes[o, b][:].bitcast(FP8X4),
-                                    lhsT_scale=q_scales[o, b][:],
-                                    rhs=key_codes[o, c][:, at:at + P].bitcast(FP4X4),
-                                    rhs_scale=key_scales[:, o * SLOTS + n:o * SLOTS + n + P],
-                                    start=(o == EARLY and at == 0), stop=(o == LATE and at + P == PIECE))
-        for b in range(BLOCKS):
-            for c in range(0, SLOTS, PIECE):
-                cols = slice(c, c + PIECE)
-                result = keep.tile([P, PIECE], F32, name=f"result{b}_{c}")
-                nc.vector.scalar_tensor_tensor(out=result[:], in0=acc[b, c][:],
-                                               scalar=ls_turned[:, P - BLOCKS + b:P - BLOCKS + b + 1],
-                                               in1=kb_all[:, cols], op0=ALU.subtract, op1=ALU.add)
-                nc.sync.dma_start(out=out[0, b * P:(b + 1) * P, cols], in_=result[:])
+        for o in (EARLY, LATE):
+            for b, c, w in pieces:
+                for n in range(c, c + w, P):
+                    nc.tensor.matmul_mx(out=acc[b, c][:, n - c:n - c + P], lhsT=q_codes[o, b][:].bitcast(FP8X4),
+                                        lhsT_scale=q_scales[o, b][:],
+                                        rhs=key_codes[o, n - n % HALF][:, n % HALF:n % HALF + P].bitcast(FP4X4),
+                                        rhs_scale=key_scales[:, o * SLOTS + n:o * SLOTS + n + P],
+                                        start=(o == EARLY and n == c), stop=(o == LATE and n + P == c + w))
+        for b, c, w in pieces:
+            result = keep.tile([P, w], F32, name=f"result{b}_{c}")
+            nc.vector.scalar_tensor_tensor(out=result[:], in0=acc[b, c][:],
+                                           scalar=ls_turned[:, P - BLOCKS + b:P - BLOCKS + b + 1],
+                                           in1=kb_all[:, c:c + w], op0=ALU.subtract, op1=ALU.add)
+            nc.sync.dma_start(out=out[0, b * P:(b + 1) * P, c:c + w], in_=result[:])

@@ -21,8 +21,8 @@ BLOCKS = NQ // P
 KB_ROW = P - 1
 HALF = SLOTS // 2
 PIECES = ((128, 128, 256), (256, 256))
-FIRST_SHARE = 56
-LATE_SHARES = (56, 96)
+FIRST_SHARE = 64
+LATE_SHARES = (64, 88)
 SCALE_ROWS = 16 * PASSES
 EARLY, LATE = 1, 0
 
@@ -37,7 +37,7 @@ def tile_attend_logprob_topk_kernel(tc, qT, k_words, k_scales, kb, ls, offs, out
 
         scale_rows = keep.tile([P, VOCAB], U8, name="scale_rows", align_bytes=64)
         nc.sync.dma_start(out=scale_rows[0:SCALE_ROWS, :].bitcast(I32),
-                          in_=k_scales.rearrange("o f t -> (o f) t").bitcast(I32))
+                          in_=k_scales.rearrange("o f t -> f o t").bitcast(I32))
         kb_row = keep.tile([P, VOCAB], F32, name="kb_row", align_bytes=64)
         nc.sync.dma_start(out=kb_row[KB_ROW:P, :], in_=kb[0:1, :])
         offsets = keep.tile([P, SLOTS // 16], U16, name="offsets")
@@ -59,20 +59,14 @@ def tile_attend_logprob_topk_kernel(tc, qT, k_words, k_scales, kb, ls, offs, out
         picked_scales = keep.tile([P, SLOTS], U8, name="picked_scales", align_bytes=64)
         nc.vector.tensor_copy(picked_scales[:], scale_rows[:].indirect(offsets[:]))
 
-        def move_scales(o):
-            for quadrant in range(4):
-                first = 16 * o + 4 * quadrant
-                nc.sync.dma_start(
-                    out=key_scales[32 * quadrant:32 * quadrant + 4, o * SLOTS:(o + 1) * SLOTS].bitcast(I32),
-                    in_=picked_scales[first:first + 4, :].bitcast(I32))
-
         q_rows = qT[0].rearrange("(o p j) q -> o p j q", o=PASSES, j=4)
         q_raw = {o: keep.tile([P, 4, NQ], F32, name=f"q_raw{o}") for o in (EARLY, LATE)}
         nc.sync.dma_start(out=q_raw[EARLY][:], in_=q_rows[EARLY])
         nc.sync.dma_start(out=ls_rows[P - BLOCKS:P, :], in_=ls[0].rearrange("(b p) o -> b (p o)", p=P))
-        move_scales(EARLY)
+        for quadrant in range(4):
+            nc.sync.dma_start(out=key_scales[32 * quadrant:32 * quadrant + 4, :].bitcast(I32),
+                              in_=picked_scales[8 * quadrant:8 * quadrant + 8, :].bitcast(I32))
         nc.sync.dma_start(out=q_raw[LATE][:], in_=q_rows[LATE])
-        move_scales(LATE)
 
         picked_kb = keep.tile([P, SLOTS], F32, name="picked_kb")
         nc.scalar.activation(picked_kb[:], kb_row[:].indirect(offsets[:]), COPY)
@@ -90,15 +84,15 @@ def tile_attend_logprob_topk_kernel(tc, qT, k_words, k_scales, kb, ls, offs, out
         ls_turned = psum.tile([P, P], F32, name="ls_turned")
         nc.tensor.transpose(ls_turned[:], ls_rows[:], ident[:])
 
-        picked_words = keep.tile([P, SLOTS], U32, name="picked_words", align_bytes=64)
+        by_pass = {}
         for c in (0, HALF):
-            nc.vector.tensor_copy(picked_words[:, c:c + HALF],
-                                  words[:].indirect(offsets[:, c // 16:(c + HALF) // 16]))
-        halves = picked_words[:].bitcast(U16).rearrange("p (n h) -> p h n", h=2)
+            picked_words = keep.tile([P, HALF], U32, name=f"picked_words{c}", align_bytes=64)
+            nc.vector.tensor_copy(picked_words[:], words[:].indirect(offsets[:, c // 16:(c + HALF) // 16]))
+            by_pass[c] = picked_words[:].bitcast(U16).rearrange("p (n h) -> p h n", h=2)
         first_codes = keep.tile([P, HALF], U16, name="first_codes", align_bytes=64)
-        other_codes = keep.tile([P, HALF + SLOTS], U16, name="other_codes", tag="ls_then_codes", align_bytes=64)
-        key_codes = {(EARLY, 0): first_codes[:], (EARLY, HALF): other_codes[:, 0:HALF],
-                     (LATE, 0): other_codes[:, HALF:SLOTS], (LATE, HALF): other_codes[:, SLOTS:SLOTS + HALF]}
+        other_codes = keep.tile([P, 3, HALF], U16, name="other_codes", tag="ls_then_codes", align_bytes=64)
+        key_codes = {(EARLY, 0): first_codes[:], (LATE, 0): other_codes[:, 2, :],
+                     (LATE, HALF): other_codes[:, LATE, :], (EARLY, HALF): other_codes[:, EARLY, :]}
 
         units = [(o, b) for o in (EARLY, LATE) for b in range(BLOCKS)]
         grouped = {u: keep.tile([P, P, 4], BF16, name=f"grouped{u[0]}{u[1]}", align_bytes=64) for u in units}
@@ -115,12 +109,12 @@ def tile_attend_logprob_topk_kernel(tc, qT, k_words, k_scales, kb, ls, offs, out
             nc.vector.quantize_mx(out=q_codes[o, b][:].bitcast(FP8X4), scales=q_scales[o, b][:],
                                   in_=grouped[o, b][:].rearrange("p w t -> p (w t)"))
 
-        nc.vector.tensor_copy(first_codes[:], halves[:, EARLY, 0:HALF])
+        nc.vector.tensor_copy(key_codes[EARLY, 0], by_pass[0][:, EARLY, :])
         cast(EARLY, 0, nc.vector.tensor_copy, 0, FIRST_SHARE)
         cast(EARLY, 0, nc.scalar.copy, FIRST_SHARE, P)
         quantize(EARLY, 0)
-        nc.vector.tensor_copy(other_codes[:, 0:HALF], halves[:, EARLY, HALF:SLOTS])
-        nc.vector.tensor_copy(other_codes[:, HALF:HALF + SLOTS], halves[:, LATE, :])
+        nc.vector.tensor_copy(other_codes[:, 0:PASSES, :], by_pass[HALF])
+        nc.vector.tensor_copy(key_codes[LATE, 0], by_pass[0][:, LATE, :])
         cast(EARLY, 1, nc.scalar.copy)
         quantize(EARLY, 1)
         for b, share in enumerate(LATE_SHARES):

@@ -117,6 +117,8 @@ def tile_attend_logprob_topk_kernel(tc, qT, k_words, k_scales, kb, ls, offs, out
         nc.vector.tensor_copy(key_codes[LATE, 0], by_pass[0][:, LATE, :])
         cast(EARLY, 1, nc.scalar.copy)
         quantize(EARLY, 1)
+        ls_cols = keep.tile([P, BLOCKS], F32, name="ls_cols")
+        nc.scalar.copy(out=ls_cols[:], in_=ls_turned[:, P - BLOCKS:P])
         for b, share in enumerate(LATE_SHARES):
             cast(LATE, b, nc.vector.tensor_copy, 0, share)
             cast(LATE, b, nc.scalar.copy, share, P)
@@ -124,15 +126,14 @@ def tile_attend_logprob_topk_kernel(tc, qT, k_words, k_scales, kb, ls, offs, out
             quantize(LATE, b)
         for o in (EARLY, LATE):
             for b, c, w in pieces:
-                for n in range(c, c + w, P):
-                    nc.tensor.matmul_mx(out=acc[b, c][:, n - c:n - c + P], lhsT=q_codes[o, b][:].bitcast(FP8X4),
-                                        lhsT_scale=q_scales[o, b][:],
-                                        rhs=key_codes[o, n - n % HALF][:, n % HALF:n % HALF + P].bitcast(FP4X4),
-                                        rhs_scale=key_scales[:, o * SLOTS + n:o * SLOTS + n + P],
-                                        start=(o == EARLY and n == c), stop=(o == LATE and n + P == c + w))
+                nc.tensor.matmul_mx(out=acc[b, c][:], lhsT=q_codes[o, b][:].bitcast(FP8X4),
+                                    lhsT_scale=q_scales[o, b][:],
+                                    rhs=key_codes[o, c - c % HALF][:, c % HALF:c % HALF + w].bitcast(FP4X4),
+                                    rhs_scale=key_scales[:, o * SLOTS + c:o * SLOTS + c + w],
+                                    start=(o == EARLY), stop=(o == LATE))
         for b, c, w in pieces:
             result = keep.tile([P, w], F32, name=f"result{b}_{c}")
             nc.vector.scalar_tensor_tensor(out=result[:], in0=acc[b, c][:],
-                                           scalar=ls_turned[:, P - BLOCKS + b:P - BLOCKS + b + 1],
+                                           scalar=ls_cols[:, b:b + 1],
                                            in1=kb_all[:, c:c + w], op0=ALU.subtract, op1=ALU.add)
             nc.sync.dma_start(out=out[0, b * P:(b + 1) * P, c:c + w], in_=result[:])

@@ -35,11 +35,11 @@ def tile_attend_logprob_topk_kernel(tc, qT, k_words, k_scales, kb, ls, offs, out
         keep = ctx.enter_context(tc.tile_pool(name="keep", bufs=1))
         psum = ctx.enter_context(tc.psum_pool(name="psum", bufs=1))
 
-        scale_rows = keep.tile([P, VOCAB], U8, name="scale_rows", align_bytes=64)
+        scale_rows = keep.tile([P, VOCAB], U8, name="scale_rows", tag="scales_then_q", align_bytes=64)
         nc.sync.dma_start(out=scale_rows[0:SCALE_ROWS, :].bitcast(I32),
                           in_=k_scales.rearrange("o f t -> f o t").bitcast(I32))
         kb_row = keep.tile([P, VOCAB], F32, name="kb_row", align_bytes=64)
-        nc.sync.dma_start(out=kb_row[KB_ROW:P, :], in_=kb[0:1, :])
+        nc.scalar.dma_start(out=kb_row[KB_ROW:P, :], in_=kb[0:1, :])
         offsets = keep.tile([P, SLOTS // 16], U16, name="offsets")
         nc.sync.dma_start(offsets[:], offs)
         words = keep.tile([P, VOCAB], U32, name="words", align_bytes=64)
@@ -49,7 +49,9 @@ def tile_attend_logprob_topk_kernel(tc, qT, k_words, k_scales, kb, ls, offs, out
         ident = keep.tile([P, P], F32, name="ident")
         make_identity(nc, ident[:])
         ls_rows = keep.tile([P, P], F32, name="ls_rows", tag="ls_then_codes", align_bytes=64)
-        nc.scalar.copy(ls_rows[0:P - BLOCKS, :], ident[0:P - BLOCKS, :])
+        zeros = keep.tile([P, P], F32, name="zeros")
+        nc.vector.memset(zeros[:], 0.0)
+        nc.scalar.copy(ls_rows[0:P - BLOCKS, :], zeros[0:P - BLOCKS, :])
 
         nc.vector.memset(kb_row[0:KB_ROW, :], 0.0)
         nc.vector.memset(scale_rows[64:P, :].bitcast(I32), 0)
@@ -60,7 +62,8 @@ def tile_attend_logprob_topk_kernel(tc, qT, k_words, k_scales, kb, ls, offs, out
         nc.vector.tensor_copy(picked_scales[:], scale_rows[:].indirect(offsets[:]))
 
         q_rows = qT[0].rearrange("(o p j) q -> o p j q", o=PASSES, j=4)
-        q_raw = {o: keep.tile([P, 4, NQ], F32, name=f"q_raw{o}") for o in (EARLY, LATE)}
+        q_raw = {EARLY: keep.tile([P, 4, NQ], F32, name="q_early"),
+                 LATE: keep.tile([P, 4, NQ], F32, name="q_late", tag="scales_then_q", align_bytes=64)}
         nc.sync.dma_start(out=q_raw[EARLY][:], in_=q_rows[EARLY])
         nc.sync.dma_start(out=ls_rows[P - BLOCKS:P, :], in_=ls[0].rearrange("(b p) o -> b (p o)", p=P))
         for quadrant in range(4):

@@ -16,15 +16,16 @@ COPY = mybir.ActivationFunctionType.Copy
 
 P = 128
 SLOTS, VOCAB, D, NQ = 512, 4096, 1024, 256
-PASSES = D // 512
-BLOCKS = NQ // P
+PACK = 4
+PASSES = D // (P * PACK)
+BANDS = NQ // P
+SCALE_ROWS = 16 * PASSES
 KB_ROW = P - 1
 HALF = SLOTS // 2
-PIECES = ((128, 128, 256), (256, 256))
-FIRST_SHARE = 64
-LATE_SHARES = (64, 88)
-SCALE_ROWS = 16 * PASSES
+EARLY_ORDER = ((0, 0, 256), (0, 256, 128), (0, 384, 128), (1, 0, 256), (1, 256, 256))
+LATE_ORDER = ((0, 256, 128), (0, 384, 128), (1, 256, 256), (0, 0, 256), (1, 0, 256))
 EARLY, LATE = 1, 0
+VECTOR_SHARE = {(EARLY, 0): 72, (EARLY, 1): 80, (LATE, 0): 80, (LATE, 1): 88}
 
 FLOPS = 2 * NQ * SLOTS * D
 
@@ -33,6 +34,7 @@ def tile_attend_logprob_topk_kernel(tc, qT, k_words, k_scales, kb, ls, offs, out
     nc = tc.nc
     with ExitStack() as ctx:
         keep = ctx.enter_context(tc.tile_pool(name="keep", bufs=1))
+        reused = ctx.enter_context(tc.tile_pool(name="reused", bufs=1))
         psum = ctx.enter_context(tc.psum_pool(name="psum", bufs=1))
 
         scale_rows = keep.tile([P, VOCAB], U8, name="scale_rows", tag="scales_then_q", align_bytes=64)
@@ -48,10 +50,10 @@ def tile_attend_logprob_topk_kernel(tc, qT, k_words, k_scales, kb, ls, offs, out
 
         ident = keep.tile([P, P], F32, name="ident")
         make_identity(nc, ident[:])
-        ls_rows = keep.tile([P, P], F32, name="ls_rows", tag="ls_then_codes", align_bytes=64)
+        ls_rows = reused.tile([P, P], F32, name="ls_rows", offset=0, align_bytes=64)
         zeros = keep.tile([P, P], F32, name="zeros")
         nc.vector.memset(zeros[:], 0.0)
-        nc.scalar.copy(ls_rows[0:P - BLOCKS, :], zeros[0:P - BLOCKS, :])
+        nc.scalar.copy(ls_rows[0:P - BANDS, :], zeros[0:P - BANDS, :])
 
         nc.vector.memset(kb_row[0:KB_ROW, :], 0.0)
         nc.vector.memset(scale_rows[64:P, :].bitcast(I32), 0)
@@ -61,11 +63,11 @@ def tile_attend_logprob_topk_kernel(tc, qT, k_words, k_scales, kb, ls, offs, out
         picked_scales = keep.tile([P, SLOTS], U8, name="picked_scales", align_bytes=64)
         nc.vector.tensor_copy(picked_scales[:], scale_rows[:].indirect(offsets[:]))
 
-        q_rows = qT[0].rearrange("(o p j) q -> o p j q", o=PASSES, j=4)
-        q_raw = {EARLY: keep.tile([P, 4, NQ], F32, name="q_early"),
-                 LATE: keep.tile([P, 4, NQ], F32, name="q_late", tag="scales_then_q", align_bytes=64)}
+        q_rows = qT[0].rearrange("(o p j) q -> o p (j q)", o=PASSES, j=PACK)
+        q_raw = {EARLY: keep.tile([P, PACK * NQ], F32, name="q_early"),
+                 LATE: keep.tile([P, PACK * NQ], F32, name="q_late", tag="scales_then_q", align_bytes=64)}
         nc.sync.dma_start(out=q_raw[EARLY][:], in_=q_rows[EARLY])
-        nc.sync.dma_start(out=ls_rows[P - BLOCKS:P, :], in_=ls[0].rearrange("(b p) o -> b (p o)", p=P))
+        nc.sync.dma_start(out=ls_rows[P - BANDS:P, :], in_=ls[0].rearrange("(b p) o -> b (p o)", p=P))
         for quadrant in range(4):
             nc.sync.dma_start(out=key_scales[32 * quadrant:32 * quadrant + 4, :].bitcast(I32),
                               in_=picked_scales[8 * quadrant:8 * quadrant + 8, :].bitcast(I32))
@@ -93,48 +95,52 @@ def tile_attend_logprob_topk_kernel(tc, qT, k_words, k_scales, kb, ls, offs, out
             nc.vector.tensor_copy(picked_words[:], words[:].indirect(offsets[:, c // 16:(c + HALF) // 16]))
             by_pass[c] = picked_words[:].bitcast(U16).rearrange("p (n h) -> p h n", h=2)
         first_codes = keep.tile([P, HALF], U16, name="first_codes", align_bytes=64)
-        other_codes = keep.tile([P, 3, HALF], U16, name="other_codes", tag="ls_then_codes", align_bytes=64)
-        key_codes = {(EARLY, 0): first_codes[:], (LATE, 0): other_codes[:, 2, :],
-                     (LATE, HALF): other_codes[:, LATE, :], (EARLY, HALF): other_codes[:, EARLY, :]}
+        second_codes = reused.tile([P, PASSES, HALF], U16, name="second_codes", offset=P, align_bytes=64)
+        last_codes = keep.tile([P, HALF], U16, name="last_codes", tag="scales_then_q", align_bytes=64)
+        key_codes = {(EARLY, 0): first_codes[:], (LATE, 0): last_codes[:],
+                     (EARLY, HALF): second_codes[:, EARLY, :], (LATE, HALF): second_codes[:, LATE, :]}
 
-        units = [(o, b) for o in (EARLY, LATE) for b in range(BLOCKS)]
-        grouped = {u: keep.tile([P, P, 4], BF16, name=f"grouped{u[0]}{u[1]}", align_bytes=64) for u in units}
+        units = [(o, b) for o in (EARLY, LATE) for b in range(BANDS)]
+        grouped = {u: keep.tile([P, P, PACK], BF16, name=f"grouped{u[0]}{u[1]}", align_bytes=64) for u in units}
         q_codes = {u: keep.tile([P, P], U32, name=f"q_codes{u[0]}{u[1]}", align_bytes=64) for u in units}
-        q_scales = {u: keep.tile([P, P], U8, name=f"q_scales{u[0]}{u[1]}", align_bytes=64) for u in units}
-        pieces = [(b, sum(widths[:k]), w) for b, widths in enumerate(PIECES) for k, w in enumerate(widths)]
-        acc = {(b, c): psum.tile([P, w], F32, name=f"acc{b}_{c}") for b, c, w in pieces}
+        q_scales = {u: keep.tile([P, P], U8, name=f"q_scales{u[0]}{u[1]}", align_bytes=64)
+                    for u in units if u != (EARLY, 1)}
+        q_scales[EARLY, 1] = reused.tile([P, P], U8, name="q_scales_held", offset=0, align_bytes=64)
+        acc = {(b, c): psum.tile([P, w], F32, name=f"acc{b}_{c}") for b, c, w in EARLY_ORDER}
 
-        def cast(o, b, copy, lo=0, hi=P):
+        def cast(o, b, copy, lo, hi):
+            rows = q_raw[o][:].rearrange("p (t q) -> p t q", t=PACK)
             copy(out=grouped[o, b][:, lo:hi, :].rearrange("p (c i) t -> p c t i", i=4),
-                 in_=q_raw[o][:, :, b * P + lo:b * P + hi].rearrange("p t (c i) -> p c t i", i=4))
+                 in_=rows[:, :, b * P + lo:b * P + hi].rearrange("p t (c i) -> p c t i", i=4))
+
+        def cast_pass(o):
+            for b in range(BANDS):
+                cast(o, b, nc.vector.tensor_copy, 0, VECTOR_SHARE[o, b])
+                cast(o, b, nc.scalar.copy, VECTOR_SHARE[o, b], P)
 
         def quantize(o, b):
             nc.vector.quantize_mx(out=q_codes[o, b][:].bitcast(FP8X4), scales=q_scales[o, b][:],
                                   in_=grouped[o, b][:].rearrange("p w t -> p (w t)"))
 
         nc.vector.tensor_copy(key_codes[EARLY, 0], by_pass[0][:, EARLY, :])
-        cast(EARLY, 0, nc.vector.tensor_copy, 0, FIRST_SHARE)
-        cast(EARLY, 0, nc.scalar.copy, FIRST_SHARE, P)
+        cast_pass(EARLY)
         quantize(EARLY, 0)
-        nc.vector.tensor_copy(other_codes[:, 0:PASSES, :], by_pass[HALF])
-        nc.vector.tensor_copy(key_codes[LATE, 0], by_pass[0][:, LATE, :])
-        cast(EARLY, 1, nc.scalar.copy)
+        nc.vector.tensor_copy(second_codes[:], by_pass[HALF])
         quantize(EARLY, 1)
-        ls_cols = keep.tile([P, BLOCKS], F32, name="ls_cols")
-        nc.scalar.copy(out=ls_cols[:], in_=ls_turned[:, P - BLOCKS:P])
-        for b, share in enumerate(LATE_SHARES):
-            cast(LATE, b, nc.vector.tensor_copy, 0, share)
-            cast(LATE, b, nc.scalar.copy, share, P)
-        for b in range(BLOCKS):
+        ls_cols = keep.tile([P, BANDS], F32, name="ls_cols")
+        nc.scalar.copy(out=ls_cols[:], in_=ls_turned[:, P - BANDS:P])
+        cast_pass(LATE)
+        for b in range(BANDS):
             quantize(LATE, b)
-        for o in (EARLY, LATE):
-            for b, c, w in pieces:
+        nc.vector.tensor_copy(key_codes[LATE, 0], by_pass[0][:, LATE, :])
+        for o, order in ((EARLY, EARLY_ORDER), (LATE, LATE_ORDER)):
+            for b, c, w in order:
                 nc.tensor.matmul_mx(out=acc[b, c][:], lhsT=q_codes[o, b][:].bitcast(FP8X4),
                                     lhsT_scale=q_scales[o, b][:],
                                     rhs=key_codes[o, c - c % HALF][:, c % HALF:c % HALF + w].bitcast(FP4X4),
                                     rhs_scale=key_scales[:, o * SLOTS + c:o * SLOTS + c + w],
                                     start=(o == EARLY), stop=(o == LATE))
-        for b, c, w in pieces:
+        for b, c, w in LATE_ORDER:
             result = keep.tile([P, w], F32, name=f"result{b}_{c}")
             nc.vector.scalar_tensor_tensor(out=result[:], in0=acc[b, c][:],
                                            scalar=ls_cols[:, b:b + 1],

@@ -22,8 +22,9 @@ BANDS = NQ // P
 SCALE_ROWS = 16 * PASSES
 KB_ROW = P - 1
 HALF = SLOTS // 2
-EARLY_ORDER = ((0, 0, 256), (0, 256, 128), (0, 384, 128), (1, 0, 256), (1, 256, 256))
-LATE_ORDER = ((0, 256, 128), (0, 384, 128), (1, 256, 256), (0, 0, 256), (1, 0, 256))
+EARLY_ORDER = ((0, 0, 256), (0, 256, 128), (0, 384, 128), (1, 0, 256), (1, 256, 128), (1, 384, 128))
+LATE_ORDER = ((0, 256, 128), (0, 384, 128), (1, 256, 128), (1, 384, 128), (0, 0, 256), (1, 0, 256))
+STORES = ((0, 256, 128), (0, 384, 128), (1, 256, 256), (0, 0, 256), (1, 0, 256))
 EARLY, LATE = 1, 0
 VECTOR_SHARE = {(EARLY, 0): 72, (EARLY, 1): 80, (LATE, 0): 80, (LATE, 1): 88}
 
@@ -68,14 +69,14 @@ def tile_attend_logprob_topk_kernel(tc, qT, k_words, k_scales, kb, ls, offs, out
                  LATE: keep.tile([P, PACK * NQ], F32, name="q_late", tag="scales_then_q", align_bytes=64)}
         nc.sync.dma_start(out=q_raw[EARLY][:], in_=q_rows[EARLY])
         nc.sync.dma_start(out=ls_rows[P - BANDS:P, :], in_=ls[0].rearrange("(b p) o -> b (p o)", p=P))
-        for quadrant in range(4):
+        for quadrant in (0, 2, 1, 3):
             nc.sync.dma_start(out=key_scales[32 * quadrant:32 * quadrant + 4, :].bitcast(I32),
                               in_=picked_scales[8 * quadrant:8 * quadrant + 8, :].bitcast(I32))
         nc.sync.dma_start(out=q_raw[LATE][:], in_=q_rows[LATE])
 
         picked_kb = keep.tile([P, SLOTS], F32, name="picked_kb")
         nc.scalar.activation(picked_kb[:], kb_row[:].indirect(offsets[:]), COPY)
-        turned = psum.tile([P, SLOTS // P, P], F32, name="turned")
+        turned = psum.tile([P, SLOTS // P, P], F32, name="turned", tag="kb_then_sums")
         for m in range(SLOTS // P):
             nc.tensor.transpose(turned[:, m, :], picked_kb[:, m * P:(m + 1) * P], ident[:])
         kb_cols = keep.tile([P, SLOTS // P], F32, name="kb_cols")
@@ -106,7 +107,9 @@ def tile_attend_logprob_topk_kernel(tc, qT, k_words, k_scales, kb, ls, offs, out
         q_scales = {u: keep.tile([P, P], U8, name=f"q_scales{u[0]}{u[1]}", align_bytes=64)
                     for u in units if u != (EARLY, 1)}
         q_scales[EARLY, 1] = reused.tile([P, P], U8, name="q_scales_held", offset=0, align_bytes=64)
-        acc = {(b, c): psum.tile([P, w], F32, name=f"acc{b}_{c}") for b, c, w in EARLY_ORDER}
+        acc = {(b, c): psum.tile([P, w], F32, name=f"acc{b}_{c}",
+                                 tag="kb_then_sums" if (b, c) == (0, 0) else f"acc{b}_{c}")
+               for b, c, w in EARLY_ORDER}
 
         def cast(o, b, copy, lo, hi):
             rows = q_raw[o][:].rearrange("p (t q) -> p t q", t=PACK)
@@ -140,9 +143,11 @@ def tile_attend_logprob_topk_kernel(tc, qT, k_words, k_scales, kb, ls, offs, out
                                     rhs=key_codes[o, c - c % HALF][:, c % HALF:c % HALF + w].bitcast(FP4X4),
                                     rhs_scale=key_scales[:, o * SLOTS + c:o * SLOTS + c + w],
                                     start=(o == EARLY), stop=(o == LATE))
-        for b, c, w in LATE_ORDER:
-            result = keep.tile([P, w], F32, name=f"result{b}_{c}")
-            nc.vector.scalar_tensor_tensor(out=result[:], in0=acc[b, c][:],
-                                           scalar=ls_cols[:, b:b + 1],
-                                           in1=kb_all[:, c:c + w], op0=ALU.subtract, op1=ALU.add)
-            nc.sync.dma_start(out=out[0, b * P:(b + 1) * P, c:c + w], in_=result[:])
+        for band, first, width in STORES:
+            result = keep.tile([P, width], F32, name=f"result{band}_{first}")
+            for b, c, w in LATE_ORDER:
+                if b == band and first <= c < first + width:
+                    nc.vector.scalar_tensor_tensor(out=result[:, c - first:c - first + w], in0=acc[b, c][:],
+                                                   scalar=ls_cols[:, b:b + 1], in1=kb_all[:, c:c + w],
+                                                   op0=ALU.subtract, op1=ALU.add)
+            nc.sync.dma_start(out=out[0, band * P:(band + 1) * P, first:first + width], in_=result[:])

@@ -40,7 +40,7 @@ def tile_attend_logprob_topk_kernel(tc, qT, k_words, k_scales, kb, ls, offs, out
 
         scale_rows = keep.tile([P, VOCAB], U8, name="scale_rows", tag="scales_then_q", align_bytes=64)
         nc.sync.dma_start(out=scale_rows[0:SCALE_ROWS, :].bitcast(I32),
-                          in_=k_scales.rearrange("o f t -> f o t").bitcast(I32))
+                          in_=k_scales.rearrange("o f t -> (o f) t").bitcast(I32))
         kb_row = keep.tile([P, VOCAB], F32, name="kb_row", align_bytes=64)
         nc.scalar.dma_start(out=kb_row[KB_ROW:P, :], in_=kb[0:1, :])
         offsets = keep.tile([P, SLOTS // 16], U16, name="offsets")
@@ -59,20 +59,25 @@ def tile_attend_logprob_topk_kernel(tc, qT, k_words, k_scales, kb, ls, offs, out
         nc.vector.memset(kb_row[0:KB_ROW, :], 0.0)
         nc.vector.memset(scale_rows[64:P, :].bitcast(I32), 0)
         nc.vector.memset(scale_rows[32:64, :].bitcast(I32), 0)
-        key_scales = keep.tile([P, PASSES * SLOTS], U8, name="key_scales", align_bytes=64)
-        nc.vector.memset(key_scales[:].bitcast(I32), 0)
+        key_scales = {o: keep.tile([P, SLOTS], U8, name=f"key_scales{o}", align_bytes=64) for o in (EARLY, LATE)}
+        for o in (EARLY, LATE):
+            nc.vector.memset(key_scales[o][:].bitcast(I32), 0)
         picked_scales = keep.tile([P, SLOTS], U8, name="picked_scales", align_bytes=64)
         nc.vector.tensor_copy(picked_scales[:], scale_rows[:].indirect(offsets[:]))
+
+        def move_scales(o):
+            for r in range(4):
+                nc.sync.dma_start(out=key_scales[o][r:P:32, :].bitcast(I32),
+                                  in_=picked_scales[16 * o + r:16 * (o + 1):4, :].bitcast(I32))
 
         q_rows = qT[0].rearrange("(o p j) q -> o p (j q)", o=PASSES, j=PACK)
         q_raw = {EARLY: keep.tile([P, PACK * NQ], F32, name="q_early"),
                  LATE: keep.tile([P, PACK * NQ], F32, name="q_late", tag="scales_then_q", align_bytes=64)}
         nc.sync.dma_start(out=q_raw[EARLY][:], in_=q_rows[EARLY])
         nc.sync.dma_start(out=ls_rows[P - BANDS:P, :], in_=ls[0].rearrange("(b p) o -> b (p o)", p=P))
-        for quadrant in (0, 2, 1, 3):
-            nc.sync.dma_start(out=key_scales[32 * quadrant:32 * quadrant + 4, :].bitcast(I32),
-                              in_=picked_scales[8 * quadrant:8 * quadrant + 8, :].bitcast(I32))
+        move_scales(EARLY)
         nc.sync.dma_start(out=q_raw[LATE][:], in_=q_rows[LATE])
+        move_scales(LATE)
 
         picked_kb = keep.tile([P, SLOTS], F32, name="picked_kb")
         nc.scalar.activation(picked_kb[:], kb_row[:].indirect(offsets[:]), COPY)
@@ -141,7 +146,7 @@ def tile_attend_logprob_topk_kernel(tc, qT, k_words, k_scales, kb, ls, offs, out
                 nc.tensor.matmul_mx(out=acc[b, c][:], lhsT=q_codes[o, b][:].bitcast(FP8X4),
                                     lhsT_scale=q_scales[o, b][:],
                                     rhs=key_codes[o, c - c % HALF][:, c % HALF:c % HALF + w].bitcast(FP4X4),
-                                    rhs_scale=key_scales[:, o * SLOTS + c:o * SLOTS + c + w],
+                                    rhs_scale=key_scales[o][:, c:c + w],
                                     start=(o == EARLY), stop=(o == LATE))
         for band, first, width in STORES:
             result = keep.tile([P, width], F32, name=f"result{band}_{first}")

@@ -65,19 +65,21 @@ def tile_attend_logprob_topk_kernel(tc, qT, k_words, k_scales, kb, ls, offs, out
         picked_scales = keep.tile([P, SLOTS], U8, name="picked_scales", align_bytes=64)
         nc.vector.tensor_copy(picked_scales[:], scale_rows[:].indirect(offsets[:]))
 
-        def move_scales(o):
-            for r in range(4):
-                nc.sync.dma_start(out=key_scales[o][r:P:32, :].bitcast(I32),
-                                  in_=picked_scales[16 * o + r:16 * (o + 1):4, :].bitcast(I32))
+        def move_scales(o, rows, lo, hi):
+            for r in rows:
+                nc.sync.dma_start(out=key_scales[o][r:P:32, lo:hi].bitcast(I32),
+                                  in_=picked_scales[16 * o + r:16 * (o + 1):4, lo:hi].bitcast(I32))
 
         q_rows = qT[0].rearrange("(o p j) q -> o p (j q)", o=PASSES, j=PACK)
         q_raw = {EARLY: keep.tile([P, PACK * NQ], F32, name="q_early"),
                  LATE: keep.tile([P, PACK * NQ], F32, name="q_late", tag="scales_then_q", align_bytes=64)}
         nc.sync.dma_start(out=q_raw[EARLY][:], in_=q_rows[EARLY])
         nc.sync.dma_start(out=ls_rows[P - BANDS:P, :], in_=ls[0].rearrange("(b p) o -> b (p o)", p=P))
-        move_scales(EARLY)
+        move_scales(EARLY, range(4), 0, SLOTS)
         nc.sync.dma_start(out=q_raw[LATE][:], in_=q_rows[LATE])
-        move_scales(LATE)
+        move_scales(LATE, range(3), HALF, SLOTS)
+        move_scales(LATE, (3,), 0, SLOTS)
+        move_scales(LATE, range(3), 0, HALF)
 
         picked_kb = keep.tile([P, SLOTS], F32, name="picked_kb")
         nc.scalar.activation(picked_kb[:], kb_row[:].indirect(offsets[:]), COPY)

@@ -25,7 +25,7 @@ HALF = SLOTS // 2
 EARLY_ORDER = ((0, 0, 256), (0, 256, 128), (0, 384, 128), (1, 0, 256), (1, 256, 128), (1, 384, 128))
 LATE_ORDER = ((0, 256, 128), (0, 384, 128), (1, 256, 128), (1, 384, 128), (0, 0, 256), (1, 0, 256))
 STORES = ((0, 256, 128), (0, 384, 128), (1, 256, 256), (0, 0, 256), (1, 0, 256))
-EARLY, LATE = 1, 0
+EARLY, LATE = 0, 1
 VECTOR_SHARE = {(EARLY, 0): 72, (EARLY, 1): 80, (LATE, 0): 80, (LATE, 1): 88}
 
 FLOPS = 2 * NQ * SLOTS * D

@@ -26,7 +26,7 @@ EARLY_ORDER = ((0, 0, 256), (0, 256, 128), (0, 384, 128), (1, 0, 256), (1, 256, 
 LATE_ORDER = ((0, 256, 128), (0, 384, 128), (1, 256, 128), (1, 384, 128), (0, 0, 256), (1, 0, 256))
 STORES = ((0, 256, 128), (0, 384, 128), (1, 256, 256), (0, 0, 256), (1, 0, 256))
 EARLY, LATE = 0, 1
-VECTOR_SHARE = {(EARLY, 0): 72, (EARLY, 1): 80, (LATE, 0): 80, (LATE, 1): 88}
+VECTOR_SHARE = {(EARLY, 0): 64, (EARLY, 1): 80, (LATE, 0): 80, (LATE, 1): 88}
 
 FLOPS = 2 * NQ * SLOTS * D
 

from contextlib import ExitStack

import concourse.mybir as mybir
from concourse.masks import make_identity

F32 = mybir.dt.float32
BF16 = mybir.dt.bfloat16
I32 = mybir.dt.int32
U32 = mybir.dt.uint32
U16 = mybir.dt.uint16
U8 = mybir.dt.uint8
FP8X4 = mybir.dt.float8_e4m3fn_x4
FP4X4 = mybir.dt.float4_e2m1fn_x4
ALU = mybir.AluOpType
COPY = mybir.ActivationFunctionType.Copy

P = 128
SLOTS, VOCAB, D, NQ = 512, 4096, 1024, 256
PACK = 4
PASSES = D // (P * PACK)
BANDS = NQ // P
SCALE_ROWS = 16 * PASSES
KB_ROW = P - 1
HALF = SLOTS // 2
EARLY_ORDER = ((0, 0, 256), (0, 256, 128), (0, 384, 128), (1, 0, 256), (1, 256, 128), (1, 384, 128))
LATE_ORDER = ((0, 256, 128), (0, 384, 128), (1, 256, 128), (1, 384, 128), (0, 0, 256), (1, 0, 256))
STORES = ((0, 256, 128), (0, 384, 128), (1, 256, 256), (0, 0, 256), (1, 0, 256))
EARLY, LATE = 0, 1
VECTOR_SHARE = {(EARLY, 0): 64, (EARLY, 1): 80, (LATE, 0): 80, (LATE, 1): 88}

FLOPS = 2 * NQ * SLOTS * D


def tile_attend_logprob_topk_kernel(tc, qT, k_words, k_scales, kb, ls, offs, out):
    nc = tc.nc
    with ExitStack() as ctx:
        keep = ctx.enter_context(tc.tile_pool(name="keep", bufs=1))
        reused = ctx.enter_context(tc.tile_pool(name="reused", bufs=1))
        psum = ctx.enter_context(tc.psum_pool(name="psum", bufs=1))

        scale_rows = keep.tile([P, VOCAB], U8, name="scale_rows", tag="scales_then_q", align_bytes=64)
        nc.sync.dma_start(out=scale_rows[0:SCALE_ROWS, :].bitcast(I32),
                          in_=k_scales.rearrange("o f t -> (o f) t").bitcast(I32))
        kb_row = keep.tile([P, VOCAB], F32, name="kb_row", align_bytes=64)
        nc.scalar.dma_start(out=kb_row[KB_ROW:P, :], in_=kb[0:1, :])
        offsets = keep.tile([P, SLOTS // 16], U16, name="offsets")
        nc.sync.dma_start(offsets[:], offs)
        words = keep.tile([P, VOCAB], U32, name="words", align_bytes=64)
        nc.sync.dma_start(out=words[:].bitcast(I32),
                          in_=k_words[0].rearrange("p t b -> p (t b)").bitcast(I32))

        ident = keep.tile([P, P], F32, name="ident")
        make_identity(nc, ident[:])
        ls_rows = reused.tile([P, P], F32, name="ls_rows", offset=0, align_bytes=64)
        zeros = keep.tile([P, P], F32, name="zeros")
        nc.vector.memset(zeros[:], 0.0)
        nc.scalar.copy(ls_rows[0:P - BANDS, :], zeros[0:P - BANDS, :])

        nc.vector.memset(kb_row[0:KB_ROW, :], 0.0)
        nc.vector.memset(scale_rows[64:P, :].bitcast(I32), 0)
        nc.vector.memset(scale_rows[32:64, :].bitcast(I32), 0)
        key_scales = {o: keep.tile([P, SLOTS], U8, name=f"key_scales{o}", align_bytes=64) for o in (EARLY, LATE)}
        for o in (EARLY, LATE):
            nc.vector.memset(key_scales[o][:].bitcast(I32), 0)
        picked_scales = keep.tile([P, SLOTS], U8, name="picked_scales", align_bytes=64)
        nc.vector.tensor_copy(picked_scales[:], scale_rows[:].indirect(offsets[:]))

        def move_scales(o, rows, lo, hi):
            for r in rows:
                nc.sync.dma_start(out=key_scales[o][r:P:32, lo:hi].bitcast(I32),
                                  in_=picked_scales[16 * o + r:16 * (o + 1):4, lo:hi].bitcast(I32))

        q_rows = qT[0].rearrange("(o p j) q -> o p (j q)", o=PASSES, j=PACK)
        q_raw = {EARLY: keep.tile([P, PACK * NQ], F32, name="q_early"),
                 LATE: keep.tile([P, PACK * NQ], F32, name="q_late", tag="scales_then_q", align_bytes=64)}
        nc.sync.dma_start(out=q_raw[EARLY][:], in_=q_rows[EARLY])
        nc.sync.dma_start(out=ls_rows[P - BANDS:P, :], in_=ls[0].rearrange("(b p) o -> b (p o)", p=P))
        move_scales(EARLY, range(4), 0, SLOTS)
        nc.sync.dma_start(out=q_raw[LATE][:], in_=q_rows[LATE])
        move_scales(LATE, range(3), HALF, SLOTS)
        move_scales(LATE, (3,), 0, SLOTS)
        move_scales(LATE, range(3), 0, HALF)

        picked_kb = keep.tile([P, SLOTS], F32, name="picked_kb")
        nc.scalar.activation(picked_kb[:], kb_row[:].indirect(offsets[:]), COPY)
        turned = psum.tile([P, SLOTS // P, P], F32, name="turned", tag="kb_then_sums")
        for m in range(SLOTS // P):
            nc.tensor.transpose(turned[:, m, :], picked_kb[:, m * P:(m + 1) * P], ident[:])
        kb_cols = keep.tile([P, SLOTS // P], F32, name="kb_cols")
        nc.scalar.copy(out=kb_cols[:], in_=turned[:, :, KB_ROW])
        spread = psum.tile([P, SLOTS], F32, name="spread")
        for m in range(SLOTS // P):
            nc.tensor.transpose(spread[:, m * P:(m + 1) * P],
                                kb_cols[:, m:m + 1].to_broadcast([P, P]), ident[:])
        kb_all = keep.tile([P, SLOTS], F32, name="kb_all")
        nc.scalar.copy(out=kb_all[:], in_=spread[:])
        ls_turned = psum.tile([P, P], F32, name="ls_turned")
        nc.tensor.transpose(ls_turned[:], ls_rows[:], ident[:])

        by_pass = {}
        for c in (0, HALF):
            picked_words = keep.tile([P, HALF], U32, name=f"picked_words{c}", align_bytes=64)
            nc.vector.tensor_copy(picked_words[:], words[:].indirect(offsets[:, c // 16:(c + HALF) // 16]))
            by_pass[c] = picked_words[:].bitcast(U16).rearrange("p (n h) -> p h n", h=2)
        first_codes = keep.tile([P, HALF], U16, name="first_codes", align_bytes=64)
        second_codes = reused.tile([P, PASSES, HALF], U16, name="second_codes", offset=P, align_bytes=64)
        last_codes = keep.tile([P, HALF], U16, name="last_codes", tag="scales_then_q", align_bytes=64)
        key_codes = {(EARLY, 0): first_codes[:], (LATE, 0): last_codes[:],
                     (EARLY, HALF): second_codes[:, EARLY, :], (LATE, HALF): second_codes[:, LATE, :]}

        units = [(o, b) for o in (EARLY, LATE) for b in range(BANDS)]
        grouped = {u: keep.tile([P, P, PACK], BF16, name=f"grouped{u[0]}{u[1]}", align_bytes=64) for u in units}
        q_codes = {u: keep.tile([P, P], U32, name=f"q_codes{u[0]}{u[1]}", align_bytes=64) for u in units}
        q_scales = {u: keep.tile([P, P], U8, name=f"q_scales{u[0]}{u[1]}", align_bytes=64)
                    for u in units if u != (EARLY, 1)}
        q_scales[EARLY, 1] = reused.tile([P, P], U8, name="q_scales_held", offset=0, align_bytes=64)
        acc = {(b, c): psum.tile([P, w], F32, name=f"acc{b}_{c}",
                                 tag="kb_then_sums" if (b, c) == (0, 0) else f"acc{b}_{c}")
               for b, c, w in EARLY_ORDER}

        def cast(o, b, copy, lo, hi):
            rows = q_raw[o][:].rearrange("p (t q) -> p t q", t=PACK)
            copy(out=grouped[o, b][:, lo:hi, :].rearrange("p (c i) t -> p c t i", i=4),
                 in_=rows[:, :, b * P + lo:b * P + hi].rearrange("p t (c i) -> p c t i", i=4))

        def cast_pass(o):
            for b in range(BANDS):
                cast(o, b, nc.vector.tensor_copy, 0, VECTOR_SHARE[o, b])
                cast(o, b, nc.scalar.copy, VECTOR_SHARE[o, b], P)

        def quantize(o, b):
            nc.vector.quantize_mx(out=q_codes[o, b][:].bitcast(FP8X4), scales=q_scales[o, b][:],
                                  in_=grouped[o, b][:].rearrange("p w t -> p (w t)"))

        nc.vector.tensor_copy(key_codes[EARLY, 0], by_pass[0][:, EARLY, :])
        cast_pass(EARLY)
        quantize(EARLY, 0)
        nc.vector.tensor_copy(second_codes[:], by_pass[HALF])
        quantize(EARLY, 1)
        ls_cols = keep.tile([P, BANDS], F32, name="ls_cols")
        nc.scalar.copy(out=ls_cols[:], in_=ls_turned[:, P - BANDS:P])
        cast_pass(LATE)
        for b in range(BANDS):
            quantize(LATE, b)
        nc.vector.tensor_copy(key_codes[LATE, 0], by_pass[0][:, LATE, :])
        for o, order in ((EARLY, EARLY_ORDER), (LATE, LATE_ORDER)):
            for b, c, w in order:
                nc.tensor.matmul_mx(out=acc[b, c][:], lhsT=q_codes[o, b][:].bitcast(FP8X4),
                                    lhsT_scale=q_scales[o, b][:],
                                    rhs=key_codes[o, c - c % HALF][:, c % HALF:c % HALF + w].bitcast(FP4X4),
                                    rhs_scale=key_scales[o][:, c:c + w],
                                    start=(o == EARLY), stop=(o == LATE))
        for band, first, width in STORES:
            result = keep.tile([P, width], F32, name=f"result{band}_{first}")
            for b, c, w in LATE_ORDER:
                if b == band and first <= c < first + width:
                    nc.vector.scalar_tensor_tensor(out=result[:, c - first:c - first + w], in0=acc[b, c][:],
                                                   scalar=ls_cols[:, b:b + 1], in1=kb_all[:, c:c + w],
                                                   op0=ALU.subtract, op1=ALU.add)
            nc.sync.dma_start(out=out[0, band * P:(band + 1) * P, first:first + width], in_=result[:])
